import numpy as np
import ml_dtypes


def mxq(x, axis, fmt="e4m3"):
    dtype, down = {"e4m3": (ml_dtypes.float8_e4m3fn, 7), "e5m2": (ml_dtypes.float8_e5m2, 14)}[fmt]
    v = np.moveaxis(np.asarray(x, np.float32).astype(ml_dtypes.bfloat16).astype(np.float64), axis, -1)
    blocks = v.reshape(v.shape[:-1] + (-1, 32))
    amax = np.abs(blocks).max(-1, keepdims=True)
    byte = np.maximum(np.where(amax > 0, np.frexp(amax)[1] - 1 + 127, 0) - down, 1)
    scale = np.exp2(byte - 127.0)
    codes = (blocks / scale).astype(np.float32).astype(dtype).astype(np.float64)
    return np.moveaxis((codes * scale).reshape(v.shape), -1, axis)


WIDE = False


def mx_kscale(k):
    if not WIDE:
        return np.ones(k)
    levels = np.array([10, -10, 5, -5, 0])
    if k % 512:
        return np.exp2(np.random.permutation(np.resize(levels, k // 32))).repeat(32)
    a = np.empty((k // 512, 16))
    for p in range(k // 512):
        a[p, :8] = np.random.permutation(np.resize(levels, 8))
        for g in range(8):
            far = levels[np.abs(levels - a[p, g]) >= 10]
            a[p, g + 8] = far[np.random.randint(len(far))]
    return np.exp2(a.ravel()).repeat(32)


def f64(x):
    return np.asarray(x).astype(np.float64)


def striped(idx):
    return np.tile(idx.reshape(-1, 16).T, (8, 1)).astype(np.uint16)


def unstriped(offs):
    return offs[:16].T.reshape(-1).astype(np.int64)


def striped8(idx):
    return np.concatenate([x.reshape(-1, 16).T for x in idx]).astype(np.uint16)


def runs(offs, k):
    lists = np.stack([offs[16 * r : 16 * r + 16].T.reshape(-1) for r in range(8)]).astype(np.int64)
    return lists[np.arange(k) % 512 // 64]


def pack_weight(w):
    k, n = w.shape
    w = f64(np.asarray(w, np.float32).astype(ml_dtypes.bfloat16)).reshape(k // 32, 32, n)
    amax = np.abs(w).max(1)
    byte = np.clip(np.where(amax > 0, np.frexp(amax)[1] - 1 + 127 - 7, 1), 1, 254)
    scaled = (w * np.exp2(127.0 - byte)[:, None, :]).reshape(k, n).astype(np.float32)
    words = np.ascontiguousarray(scaled.reshape(k // 512, 128, 4, n).transpose(0, 1, 3, 2)).astype(ml_dtypes.float8_e4m3fn).view(np.uint8)
    return words, np.ascontiguousarray(byte.astype(np.uint8).reshape(k // 512, 16, n))


def unpack_weight(words, scales):
    g, p, n, _ = words.shape
    vals = np.ascontiguousarray(words).view(ml_dtypes.float8_e4m3fn).astype(np.float64) * np.repeat(np.exp2(scales.astype(np.float64) - 127.0), 8, axis=1)[..., None]
    return vals.transpose(0, 1, 3, 2).reshape(g * 512, n)


E2M1 = np.array([0.0, 0.5, 1.0, 1.5, 2.0, 3.0, 4.0, 6.0, -0.0, -0.5, -1.0, -1.5, -2.0, -3.0, -4.0, -6.0])


def pack_fp4(w):
    k, n = w.shape
    w = f64(np.asarray(w, np.float32).astype(ml_dtypes.bfloat16)).reshape(k // 32, 32, n)
    amax = np.abs(w).max(1)
    mant, ex = np.frexp(amax / 6.0)
    byte = np.clip(np.where(amax > 0, np.where(mant > 0.5, ex, ex - 1) + 127, 1), 1, 254)
    scaled = (w * np.exp2(127.0 - byte)[:, None, :]).reshape(k, n).astype(np.float32)
    c = np.ascontiguousarray(scaled.reshape(k // 512, 128, 4, n).transpose(0, 1, 3, 2)).astype(ml_dtypes.float4_e2m1fn).view(np.uint8) & 0xF
    words = (c[..., 0::2] | (c[..., 1::2] << 4)).reshape(k // 512, 128, 2 * n)
    return np.ascontiguousarray(words), np.ascontiguousarray(byte.astype(np.uint8).reshape(k // 512, 16, n))


def unpack_fp4(words, scales):
    g, _, n = scales.shape
    words = np.ascontiguousarray(words).reshape(g, 128, n, 2)
    nib = np.empty((g, 128, n, 4), np.uint8)
    nib[..., 0::2] = words & 0xF
    nib[..., 1::2] = words >> 4
    vals = E2M1[nib] * np.repeat(np.exp2(scales.astype(np.float64) - 127.0), 8, axis=1)[..., None]
    return vals.transpose(0, 1, 3, 2).reshape(g * 512, n)


def planes(y):
    n, m = y.shape
    v = y.astype(np.float32).astype(ml_dtypes.bfloat16).astype(np.float64).reshape(n // 32, 32, m)
    top = np.abs(v).max(1)
    byte = np.clip(np.where(top > 0, np.frexp(top)[1] - 1 + 127 - 7, 1), 1, 254)
    codes = (v * np.exp2(127.0 - byte)[:, None, :]).reshape(n, m).astype(np.float32).astype(ml_dtypes.float8_e4m3fn).view(np.uint8)
    words = codes.reshape(n // 512, 128, 4, m).transpose(0, 1, 3, 2)
    return np.ascontiguousarray(words), np.ascontiguousarray(byte.astype(np.uint8).reshape(n // 512, 16, m))


K, T, S, V, N, H = 512, 2048, 512, 256, 512, 512


def setup_inputs():
    n = np.random.standard_normal
    s = mx_kscale(K)[:, None]
    u = mx_kscale(H)
    packed_xT = pack_weight(n((K, T)) * s)
    packed_w1 = pack_fp4(n((K, H)) / np.sqrt(K) / s)
    packed_w3 = pack_fp4(n((H, N)) / np.sqrt(H) / u[:, None])
    return {
        "x_words": packed_xT[0],
        "x_scales": packed_xT[1],
        "w1_words": packed_w1[0],
        "w1_scales": packed_w1[1],
        "w2": (n((K, H)) / np.sqrt(K) / s * u).astype(np.float32),
        "w3_words": packed_w3[0],
        "w3_scales": packed_w3[1],
        "offs": striped(np.random.permutation(T)[:S]),
        "p1": striped8(np.stack([np.random.permutation(S)[:V] for _ in range(8)])),
        "p2": striped8(np.stack([np.random.permutation(S)[:V] for _ in range(8)])),
        "p3": striped8(np.stack([np.random.permutation(S)[:V] for _ in range(8)])),
    }


def reference(x_words, x_scales, w1_words, w1_scales, w2, w3_words, w3_scales, offs, p1, p2, p3):
    xq = unpack_weight(x_words, x_scales)[:, unstriped(offs)]
    s = unpack_fp4(w1_words, w1_scales).T @ xq
    e1 = np.exp(s[np.arange(H)[:, None], runs(p1, H)])
    val = mxq(f64(w2), 0, "e4m3").T @ xq
    e2 = np.exp(s[np.arange(H)[:, None], runs(p2, H)])
    e3 = np.exp(s[np.arange(H)[:, None], runs(p3, H)])
    z = (e1 * (val[np.arange(H)[:, None], runs(p1, H)]) + e2 * (val[np.arange(H)[:, None], runs(p2, H)]) + e3 * (val[np.arange(H)[:, None], runs(p3, H)])) / (e1 + e2 + e3)
    out_0 = unpack_fp4(w3_words, w3_scales).T @ mxq(z, 0, "e4m3")
    return (out_0,) + planes(out_0)

@@ -1,0 +1,214 @@
+from contextlib import ExitStack
+
+import concourse.mybir as mybir
+from concourse.masks import make_identity
+
+K, T, S, V, N, H = 512, 2048, 512, 256, 512, 512
+FLOPS = 2 * K * H * S * 2 + 2 * H * N * V
+
+F32 = mybir.dt.float32
+BF16 = mybir.dt.bfloat16
+I32 = mybir.dt.int32
+U32 = mybir.dt.uint32
+U16 = mybir.dt.uint16
+U8 = mybir.dt.uint8
+FP8X4 = mybir.dt.float8_e4m3fn_x4
+FP4X4 = mybir.dt.float4_e2m1fn_x4
+ACT = mybir.ActivationFunctionType
+MULT = mybir.AluOpType.mult
+
+P = 128
+PACK = 4
+VH = 128
+HALVES = V // VH
+
+
+def load_scale_rows(queues, plane, rows):
+    for q in range(4):
+        queues[q].dma_start(out=plane[32 * q : 32 * q + 4, :].bitcast(I32), in_=rows[4 * q : 4 * q + 4, :].bitcast(I32))
+
+
+def deal_words(nc, dealt, raw):
+    nc.vector.tensor_copy(
+        out=dealt[:].rearrange("p (t a m b) -> p a t m b", t=4, m=8, b=2),
+        in_=raw[:].rearrange("p (a m t b) -> p a t m b", t=4, m=8, b=2),
+    )
+
+
+def deal_scales(nc, dealt, raw):
+    nc.vector.tensor_copy(
+        out=dealt[:].rearrange("p (t a m) -> p a t m", t=4, m=16),
+        in_=raw[:].rearrange("p (a m t) -> p a t m", t=4, m=16),
+    )
+
+
+def tile_picked_aftlocal_none_po_kernel(
+    tc, x_words, x_scales, w1_words, w1_scales, w2, w3_words, w3_scales, offs, p1, p2, p3, out_0, out_1, out_2
+):
+    nc = tc.nc
+    with ExitStack() as ctx:
+        keep = ctx.enter_context(tc.tile_pool(name="keep", bufs=1))
+        sums = ctx.enter_context(tc.psum_pool(name="sums", bufs=1))
+        ring = ctx.enter_context(tc.psum_pool(name="ring", bufs=4))
+
+        offs_t = keep.tile([P, S // 16], U16, name="offs_t")
+        lists = [keep.tile([P, V // 16], U16, name="list%d" % k) for k in range(3)]
+        xw = keep.tile([P, T], U32, name="xw", align_bytes=64)
+        xs = keep.tile([P, T], U8, name="xs", align_bytes=64)
+        ww_raw = keep.tile([P, 2 * H], U8, name="ww_raw", align_bytes=64)
+        ws_raw = keep.tile([P, H], U8, name="ws_raw", align_bytes=64)
+        w2_raw = [keep.tile([P, PACK, H // 2], F32, name="w2_raw%d" % a, align_bytes=64) for a in range(2)]
+        ident = keep.tile([P, P], F32, name="ident", align_bytes=64)
+
+        nc.vector.memset(xs[:].bitcast(I32), 0)
+        nc.gpsimd.memset(ws_raw[:].bitcast(I32), 0)
+
+        nc.sync.dma_start(offs_t[:], offs)
+        nc.sync.dma_start(lists[0][:], p1)
+        nc.sync.dma_start(out=xw[:].bitcast(I32), in_=x_words[0].rearrange("p n t -> p (n t)").bitcast(I32))
+        nc.scalar.dma_start(out=ww_raw[:].bitcast(I32), in_=w1_words[0].bitcast(I32))
+        load_scale_rows([nc.scalar] * 4, xs, x_scales[0])
+        load_scale_rows([nc.scalar, nc.scalar, nc.gpsimd, nc.gpsimd], ws_raw, w1_scales[0])
+        w2_rows = w2.rearrange("(p j) c -> p j c", j=PACK)
+        for a in range(2):
+            nc.sync.dma_start(out=w2_raw[a][:], in_=w2_rows[:, :, a * (H // 2) : (a + 1) * (H // 2)])
+        nc.sync.dma_start(lists[1][:], p2)
+        nc.sync.dma_start(lists[2][:], p3)
+        make_identity(nc, ident[:])
+
+        xg_s = keep.tile([P, S], U8, name="xg_s", align_bytes=64)
+        xg_w = keep.tile([P, S], U32, name="xg_w", align_bytes=64)
+        w1w = keep.tile([P, 2 * H], U8, name="w1w", align_bytes=64)
+        w1s = keep.tile([P, H], U8, name="w1s", align_bytes=64)
+        w3w = keep.tile([P, 2 * N], U8, name="w3w", align_bytes=64)
+        w3s = keep.tile([P, N], U8, name="w3s", align_bytes=64)
+        nc.vector.tensor_copy(xg_s[:], xs[:].indirect(offs_t[:]))
+        deal_words(nc, w1w, ww_raw)
+        nc.vector.tensor_copy(xg_w[:], xw[:].indirect(offs_t[:]))
+        deal_scales(nc, w1s, ws_raw)
+        nc.sync.dma_start(out=ww_raw[:].bitcast(I32), in_=w3_words[0].bitcast(I32))
+        load_scale_rows([nc.sync] * 4, ws_raw, w3_scales[0])
+
+        s_sb = []
+        for t in range(PACK):
+            bank = ring.tile([P, S], F32, name="bank")
+            nc.tensor.matmul_mx(
+                out=bank[:],
+                lhsT=w1w[:, 256 * t : 256 * (t + 1)].bitcast(FP4X4),
+                lhsT_scale=w1s[:, P * t : P * (t + 1)],
+                rhs=xg_w[:].bitcast(FP8X4),
+                rhs_scale=xg_s[:],
+                start=True,
+                stop=True,
+            )
+            s_t = keep.tile([P, S], F32, name="s%d" % t, align_bytes=64)
+            nc.scalar.copy(out=s_t[:], in_=bank[:])
+            s_sb.append(s_t)
+
+        w2_bf = keep.tile([P, PACK, P, PACK], BF16, name="w2_bf", align_bytes=64)
+        w2q = keep.tile([P, H], U32, name="w2q", align_bytes=64)
+        w2s = keep.tile([P, H], U8, name="w2s", align_bytes=64)
+        for a in range(2):
+            nc.vector.tensor_copy(
+                out=w2_bf[:, :, 64 * a : 64 * (a + 1), :].rearrange("p t m j -> p m t j"),
+                in_=w2_raw[a][:].rearrange("p j (m t) -> p m t j", t=PACK),
+            )
+        for t in range(PACK):
+            nc.vector.quantize_mx(
+                out=w2q[:, P * t : P * (t + 1)].bitcast(FP8X4),
+                scales=w2s[:, P * t : P * (t + 1)],
+                in_=w2_bf[:, t, :, :].rearrange("p m j -> p (m j)"),
+            )
+
+        den = [sums.tile([P, PACK, P], F32, name="den%d" % h) for h in range(HALVES)]
+        num = [sums.tile([P, PACK, P], F32, name="num%d" % h) for h in range(HALVES)]
+
+        def add_turned(acc, terms):
+            for k in range(3):
+                nc.tensor.matmul(acc, terms[k], ident[:], start=(k == 0), stop=(k == 2), is_transpose=True)
+
+        for t in range(PACK):
+            bank = ring.tile([P, S], F32, name="bank")
+            nc.tensor.matmul_mx(
+                out=bank[:],
+                lhsT=w2q[:, P * t : P * (t + 1)].bitcast(FP8X4),
+                lhsT_scale=w2s[:, P * t : P * (t + 1)],
+                rhs=xg_w[:].bitcast(FP8X4),
+                rhs_scale=xg_s[:],
+                start=True,
+                stop=True,
+            )
+            val_t = keep.tile([P, S], F32, name="val%d" % t, align_bytes=64)
+            nc.vector.tensor_copy(out=val_t[:], in_=bank[:])
+            e = [keep.tile([P, V], F32, name="e%d_%d" % (t, k), align_bytes=64) for k in range(3)]
+            ev = [keep.tile([P, V], F32, name="ev%d_%d" % (t, k), align_bytes=64) for k in range(3)]
+            for k in range(3):
+                nc.scalar.activation(e[k][:], s_sb[t][:].indirect(lists[k][:]), ACT.Exp)
+            for h in range(HALVES):
+                add_turned(den[h][:, t, :], [e[k][:, VH * h : VH * (h + 1)] for k in range(3)])
+            for k in range(3):
+                nc.vector.tensor_tensor(ev[k][:], val_t[:].indirect(lists[k][:]), e[k][:], MULT)
+            for h in range(HALVES):
+                add_turned(num[h][:, t, :], [ev[k][:, VH * h : VH * (h + 1)] for k in range(3)])
+
+        deal_words(nc, w3w, ww_raw)
+        deal_scales(nc, w3s, ws_raw)
+
+        y_words = keep.tile([P, V], U32, name="y_words", align_bytes=64)
+        y_scales = keep.tile([P, V], U8, name="y_scales", align_bytes=64)
+        out_rows = out_0.rearrange("(p t) v -> p t v", t=PACK)
+        out_words = out_1[0].rearrange("p v r -> p (v r)").bitcast(I32)
+        for h in range(HALVES):
+            cols = slice(VH * h, VH * (h + 1))
+            root = keep.tile([P, H], F32, name="root%d" % h, align_bytes=64)
+            inv = keep.tile([P, H], F32, name="inv%d" % h, align_bytes=64)
+            nc.scalar.activation(
+                root[:].rearrange("v (u p e) -> v u p e", u=2, e=2),
+                den[h][:].rearrange("v (u e) p -> v u p e", e=2),
+                ACT.Abs_reciprocal_sqrt,
+            )
+            nc.scalar.activation(inv[:], root[:], ACT.Square)
+            z_t = keep.tile([P, H], BF16, name="z_t%d" % h, align_bytes=64)
+            nc.vector.tensor_tensor(
+                z_t[:].rearrange("v (u p e) -> v u p e", u=2, e=2),
+                num[h][:].rearrange("v (u e) p -> v u p e", e=2),
+                inv[:].rearrange("v (u p e) -> v u p e", u=2, e=2),
+                MULT,
+            )
+            turned = ring.tile([P, S], F32, name="bank")
+            z_pairs = z_t[:].bitcast(F32)
+            for u in range(2):
+                nc.tensor.transpose(turned[:, P * u : P * (u + 1)], z_pairs[:, P * u : P * (u + 1)], ident[:])
+            z_bf = keep.tile([P, VH * PACK], BF16, name="z_bf%d" % h, align_bytes=64)
+            nc.scalar.copy(
+                out=z_bf[:].bitcast(F32).rearrange("p (v u) -> p v u", u=2),
+                in_=turned[:, 0 : 2 * P].rearrange("p (u v) -> p v u", u=2),
+            )
+            zq = keep.tile([P, VH], U32, name="zq%d" % h, align_bytes=64)
+            zs = keep.tile([P, VH], U8, name="zs%d" % h, align_bytes=64)
+            nc.vector.quantize_mx(out=zq[:].bitcast(FP8X4), scales=zs[:], in_=z_bf[:])
+            bank = ring.tile([P, S], F32, name="bank")
+            for t in range(PACK):
+                nc.tensor.matmul_mx(
+                    out=bank[:, VH * t : VH * (t + 1)],
+                    lhsT=w3w[:, 256 * t : 256 * (t + 1)].bitcast(FP4X4),
+                    lhsT_scale=w3s[:, P * t : P * (t + 1)],
+                    rhs=zq[:].bitcast(FP8X4),
+                    rhs_scale=zs[:],
+                    start=True,
+                    stop=True,
+                )
+            y = keep.tile([P, PACK, VH], F32, name="y%d" % h, align_bytes=64)
+            nc.scalar.copy(out=y[:].rearrange("p t v -> p (t v)"), in_=bank[:])
+            nc.sync.dma_start(out=out_rows[:, :, cols], in_=y[:])
+            y_bf = keep.tile([P, VH, PACK], BF16, name="y_bf%d" % h, align_bytes=64)
+            nc.vector.tensor_copy(out=y_bf[:], in_=y[:].rearrange("p t v -> p v t"))
+            nc.vector.quantize_mx(
+                out=y_words[:, cols].bitcast(FP8X4), scales=y_scales[:, cols], in_=y_bf[:].rearrange("p v t -> p (v t)")
+            )
+            nc.sync.dma_start(out=out_words[:, cols], in_=y_words[:, cols].bitcast(I32))
+        for q in range(4):
+            queue = nc.sync if q % 2 == 0 else nc.scalar
+            queue.dma_start(
+                out=out_2[0][4 * q : 4 * q + 4, :].bitcast(I32), in_=y_scales[32 * q : 32 * q + 4, :].bitcast(I32)
+            )

@@ -48,27 +48,32 @@ def tile_picked_aftlocal_none_po_kernel(
     nc = tc.nc
     with ExitStack() as ctx:
         keep = ctx.enter_context(tc.tile_pool(name="keep", bufs=1))
-        sums = ctx.enter_context(tc.psum_pool(name="sums", bufs=1))
-        ring = ctx.enter_context(tc.psum_pool(name="ring", bufs=4))
+        psum = ctx.enter_context(tc.psum_pool(name="psum", bufs=1))
+
+        def in_bank(b, name):
+            return psum.tile([P, S], F32, name=name, tag="bank%d" % b)
 
         offs_t = keep.tile([P, S // 16], U16, name="offs_t")
         lists = [keep.tile([P, V // 16], U16, name="list%d" % k) for k in range(3)]
         xw = keep.tile([P, T], U32, name="xw", align_bytes=64)
         xs = keep.tile([P, T], U8, name="xs", align_bytes=64)
         ww_raw = keep.tile([P, 2 * H], U8, name="ww_raw", align_bytes=64)
+        w3w_raw = keep.tile([P, 2 * N], U8, name="w3w_raw", align_bytes=64)
         ws_raw = keep.tile([P, H], U8, name="ws_raw", align_bytes=64)
         w2_raw = [keep.tile([P, PACK, H // 2], F32, name="w2_raw%d" % a, align_bytes=64) for a in range(2)]
         ident = keep.tile([P, P], F32, name="ident", align_bytes=64)
 
-        nc.vector.memset(xs[:].bitcast(I32), 0)
+        nc.vector.memset(xs[:, 0 : T // 2].bitcast(I32), 0)
+        nc.gpsimd.memset(xs[:, T // 2 : T].bitcast(I32), 0)
         nc.gpsimd.memset(ws_raw[:].bitcast(I32), 0)
 
         nc.sync.dma_start(offs_t[:], offs)
-        nc.sync.dma_start(lists[0][:], p1)
+        nc.sync.dma_start(out=ww_raw[:].bitcast(I32), in_=w1_words[0].bitcast(I32))
+        nc.sync.dma_start(out=w3w_raw[:].bitcast(I32), in_=w3_words[0].bitcast(I32))
+        load_scale_rows([nc.sync] * 4, xs, x_scales[0])
         nc.sync.dma_start(out=xw[:].bitcast(I32), in_=x_words[0].rearrange("p n t -> p (n t)").bitcast(I32))
-        nc.scalar.dma_start(out=ww_raw[:].bitcast(I32), in_=w1_words[0].bitcast(I32))
-        load_scale_rows([nc.scalar] * 4, xs, x_scales[0])
-        load_scale_rows([nc.scalar, nc.scalar, nc.gpsimd, nc.gpsimd], ws_raw, w1_scales[0])
+        load_scale_rows([nc.sync] * 4, ws_raw, w1_scales[0])
+        nc.sync.dma_start(lists[0][:], p1)
         w2_rows = w2.rearrange("(p j) c -> p j c", j=PACK)
         for a in range(2):
             nc.sync.dma_start(out=w2_raw[a][:], in_=w2_rows[:, :, a * (H // 2) : (a + 1) * (H // 2)])
@@ -84,26 +89,29 @@ def tile_picked_aftlocal_none_po_kernel(
         w3s = keep.tile([P, N], U8, name="w3s", align_bytes=64)
         nc.vector.tensor_copy(xg_s[:], xs[:].indirect(offs_t[:]))
         deal_words(nc, w1w, ww_raw)
+        deal_words(nc, w3w, w3w_raw)
         nc.vector.tensor_copy(xg_w[:], xw[:].indirect(offs_t[:]))
         deal_scales(nc, w1s, ws_raw)
-        nc.sync.dma_start(out=ww_raw[:].bitcast(I32), in_=w3_words[0].bitcast(I32))
         load_scale_rows([nc.sync] * 4, ws_raw, w3_scales[0])
 
-        s_sb = []
-        for t in range(PACK):
-            bank = ring.tile([P, S], F32, name="bank")
+        def project(bank, codes, scales):
             nc.tensor.matmul_mx(
                 out=bank[:],
-                lhsT=w1w[:, 256 * t : 256 * (t + 1)].bitcast(FP4X4),
-                lhsT_scale=w1s[:, P * t : P * (t + 1)],
+                lhsT=codes,
+                lhsT_scale=scales,
                 rhs=xg_w[:].bitcast(FP8X4),
                 rhs_scale=xg_s[:],
                 start=True,
                 stop=True,
             )
-            s_t = keep.tile([P, S], F32, name="s%d" % t, align_bytes=64)
-            nc.scalar.copy(out=s_t[:], in_=bank[:])
-            s_sb.append(s_t)
+            return bank
+
+        s_banks = [
+            project(in_bank(t, "s_acc"), w1w[:, 256 * t : 256 * (t + 1)].bitcast(FP4X4), w1s[:, P * t : P * (t + 1)])
+            for t in range(PACK)
+        ]
+        s_sb = [keep.tile([P, S], F32, name="s%d" % t, align_bytes=64) for t in range(PACK)]
+        nc.scalar.copy(out=s_sb[0][:], in_=s_banks[0][:])
 
         w2_bf = keep.tile([P, PACK, P, PACK], BF16, name="w2_bf", align_bytes=64)
         w2q = keep.tile([P, H], U32, name="w2q", align_bytes=64)
@@ -120,38 +128,41 @@ def tile_picked_aftlocal_none_po_kernel(
                 in_=w2_bf[:, t, :, :].rearrange("p m j -> p (m j)"),
             )
 
-        den = [sums.tile([P, PACK, P], F32, name="den%d" % h) for h in range(HALVES)]
-        num = [sums.tile([P, PACK, P], F32, name="num%d" % h) for h in range(HALVES)]
+        val_banks = [
+            project(in_bank(4 + t, "val_acc"), w2q[:, P * t : P * (t + 1)].bitcast(FP8X4), w2s[:, P * t : P * (t + 1)])
+            for t in range(PACK)
+        ]
 
         def add_turned(acc, terms):
             for k in range(3):
                 nc.tensor.matmul(acc, terms[k], ident[:], start=(k == 0), stop=(k == 2), is_transpose=True)
 
+        den = [in_bank(h, "den") for h in range(HALVES)]
+        num = [in_bank(2 + h, "num") for h in range(HALVES)]
         for t in range(PACK):
-            bank = ring.tile([P, S], F32, name="bank")
-            nc.tensor.matmul_mx(
-                out=bank[:],
-                lhsT=w2q[:, P * t : P * (t + 1)].bitcast(FP8X4),
-                lhsT_scale=w2s[:, P * t : P * (t + 1)],
-                rhs=xg_w[:].bitcast(FP8X4),
-                rhs_scale=xg_s[:],
-                start=True,
-                stop=True,
-            )
-            val_t = keep.tile([P, S], F32, name="val%d" % t, align_bytes=64)
-            nc.vector.tensor_copy(out=val_t[:], in_=bank[:])
             e = [keep.tile([P, V], F32, name="e%d_%d" % (t, k), align_bytes=64) for k in range(3)]
             ev = [keep.tile([P, V], F32, name="ev%d_%d" % (t, k), align_bytes=64) for k in range(3)]
             for k in range(3):
                 nc.scalar.activation(e[k][:], s_sb[t][:].indirect(lists[k][:]), ACT.Exp)
+            if t + 1 < PACK:
+                nc.scalar.copy(out=s_sb[t + 1][:], in_=s_banks[t + 1][:])
+            val_t = keep.tile([P, S], F32, name="val%d" % t, align_bytes=64)
+            nc.vector.tensor_copy(out=val_t[:], in_=val_banks[t][:])
             for h in range(HALVES):
-                add_turned(den[h][:, t, :], [e[k][:, VH * h : VH * (h + 1)] for k in range(3)])
-            for k in range(3):
-                nc.vector.tensor_tensor(ev[k][:], val_t[:].indirect(lists[k][:]), e[k][:], MULT)
-            for h in range(HALVES):
-                add_turned(num[h][:, t, :], [ev[k][:, VH * h : VH * (h + 1)] for k in range(3)])
+                add_turned(den[h][:, P * t : P * (t + 1)], [e[k][:, VH * h : VH * (h + 1)] for k in range(3)])
+            if t + 1 < PACK:
+                for k in range(3):
+                    nc.vector.tensor_tensor(ev[k][:], val_t[:].indirect(lists[k][:]), e[k][:], MULT)
+                for h in range(HALVES):
+                    add_turned(num[h][:, P * t : P * (t + 1)], [ev[k][:, VH * h : VH * (h + 1)] for k in range(3)])
+            else:
+                for h in range(HALVES):
+                    cols = slice(VH * h, VH * (h + 1))
+                    for k in range(3):
+                        offsets = lists[k][:, VH // 16 * h : VH // 16 * (h + 1)]
+                        nc.vector.tensor_tensor(ev[k][:, cols], val_t[:].indirect(offsets), e[k][:, cols], MULT)
+                    add_turned(num[h][:, P * t : P * (t + 1)], [ev[k][:, cols] for k in range(3)])
 
-        deal_words(nc, w3w, ww_raw)
         deal_scales(nc, w3s, ws_raw)
 
         y_words = keep.tile([P, V], U32, name="y_words", align_bytes=64)
@@ -164,18 +175,18 @@ def tile_picked_aftlocal_none_po_kernel(
             inv = keep.tile([P, H], F32, name="inv%d" % h, align_bytes=64)
             nc.scalar.activation(
                 root[:].rearrange("v (u p e) -> v u p e", u=2, e=2),
-                den[h][:].rearrange("v (u e) p -> v u p e", e=2),
+                den[h][:].rearrange("v (u e p) -> v u p e", u=2, e=2),
                 ACT.Abs_reciprocal_sqrt,
             )
             nc.scalar.activation(inv[:], root[:], ACT.Square)
             z_t = keep.tile([P, H], BF16, name="z_t%d" % h, align_bytes=64)
             nc.vector.tensor_tensor(
                 z_t[:].rearrange("v (u p e) -> v u p e", u=2, e=2),
-                num[h][:].rearrange("v (u e) p -> v u p e", e=2),
+                num[h][:].rearrange("v (u e p) -> v u p e", u=2, e=2),
                 inv[:].rearrange("v (u p e) -> v u p e", u=2, e=2),
                 MULT,
             )
-            turned = ring.tile([P, S], F32, name="bank")
+            turned = in_bank(4 + h, "turned")
             z_pairs = z_t[:].bitcast(F32)
             for u in range(2):
                 nc.tensor.transpose(turned[:, P * u : P * (u + 1)], z_pairs[:, P * u : P * (u + 1)], ident[:])
@@ -187,19 +198,24 @@ def tile_picked_aftlocal_none_po_kernel(
             zq = keep.tile([P, VH], U32, name="zq%d" % h, align_bytes=64)
             zs = keep.tile([P, VH], U8, name="zs%d" % h, align_bytes=64)
             nc.vector.quantize_mx(out=zq[:].bitcast(FP8X4), scales=zs[:], in_=z_bf[:])
-            bank = ring.tile([P, S], F32, name="bank")
-            for t in range(PACK):
-                nc.tensor.matmul_mx(
-                    out=bank[:, VH * t : VH * (t + 1)],
-                    lhsT=w3w[:, 256 * t : 256 * (t + 1)].bitcast(FP4X4),
-                    lhsT_scale=w3s[:, P * t : P * (t + 1)],
-                    rhs=zq[:].bitcast(FP8X4),
-                    rhs_scale=zs[:],
-                    start=True,
-                    stop=True,
-                )
             y = keep.tile([P, PACK, VH], F32, name="y%d" % h, align_bytes=64)
-            nc.scalar.copy(out=y[:].rearrange("p t v -> p (t v)"), in_=bank[:])
+            for u in range(2):
+                bank = in_bank((6 + 2 * h + u) % 8, "y_acc")
+                for t in range(2 * u, 2 * u + 2):
+                    nc.tensor.matmul_mx(
+                        out=bank[:, VH * (t % 2) : VH * (t % 2 + 1)],
+                        lhsT=w3w[:, 256 * t : 256 * (t + 1)].bitcast(FP4X4),
+                        lhsT_scale=w3s[:, P * t : P * (t + 1)],
+                        rhs=zq[:].bitcast(FP8X4),
+                        rhs_scale=zs[:],
+                        start=True,
+                        stop=True,
+                    )
+                y_pair = y[:, 2 * u : 2 * u + 2, :].rearrange("p t v -> p (t v)")
+                if u == 0:
+                    nc.scalar.copy(out=y_pair, in_=bank[:, 0 : 2 * VH])
+                else:
+                    nc.vector.tensor_copy(out=y_pair, in_=bank[:, 0 : 2 * VH])
             nc.sync.dma_start(out=out_rows[:, :, cols], in_=y[:])
             y_bf = keep.tile([P, VH, PACK], BF16, name="y_bf%d" % h, align_bytes=64)
             nc.vector.tensor_copy(out=y_bf[:], in_=y[:].rearrange("p t v -> p v t"))

@@ -19,26 +19,35 @@ MULT = mybir.AluOpType.mult
 
 P = 128
 PACK = 4
-VH = 128
-HALVES = V // VH
+LISTS = 3
+QUADRANTS = 4
+STRIPE = 16
+HALVES = V // P
+
+S_BANKS = (0, 1, 2, 3)
+VAL_BANKS = (4, 5, 6, 7)
+DEN_BANKS = (4, 5)
+NUM_BANKS = (0, 1)
+TURN_BANKS = (2, 3)
+Y_BANKS = ((6, 7), (4, 5))
 
 
-def load_scale_rows(queues, plane, rows):
-    for q in range(4):
-        queues[q].dma_start(out=plane[32 * q : 32 * q + 4, :].bitcast(I32), in_=rows[4 * q : 4 * q + 4, :].bitcast(I32))
+def load_scale_rows(nc, plane, rows):
+    for q in range(QUADRANTS):
+        nc.sync.dma_start(out=plane[32 * q : 32 * q + 4, :].bitcast(I32), in_=rows[4 * q : 4 * q + 4, :].bitcast(I32))
 
 
 def deal_words(nc, dealt, raw):
     nc.vector.tensor_copy(
-        out=dealt[:].rearrange("p (t a m b) -> p a t m b", t=4, m=8, b=2),
-        in_=raw[:].rearrange("p (a m t b) -> p a t m b", t=4, m=8, b=2),
+        out=dealt[:].rearrange("p (t a m b) -> p a t m b", t=PACK, m=8, b=2),
+        in_=raw[:].rearrange("p (a m t b) -> p a t m b", t=PACK, m=8, b=2),
     )
 
 
 def deal_scales(nc, dealt, raw):
     nc.vector.tensor_copy(
-        out=dealt[:].rearrange("p (t a m) -> p a t m", t=4, m=16),
-        in_=raw[:].rearrange("p (a m t) -> p a t m", t=4, m=16),
+        out=dealt[:].rearrange("p (t a m) -> p a t m", t=PACK, m=16),
+        in_=raw[:].rearrange("p (a m t) -> p a t m", t=PACK, m=16),
     )
 
 
@@ -53,30 +62,32 @@ def tile_picked_aftlocal_none_po_kernel(
         def in_bank(b, name):
             return psum.tile([P, S], F32, name=name, tag="bank%d" % b)
 
-        offs_t = keep.tile([P, S // 16], U16, name="offs_t")
-        lists = [keep.tile([P, V // 16], U16, name="list%d" % k) for k in range(3)]
+        def tile_cols(t, width=P):
+            return slice(width * t, width * (t + 1))
+
+        offs_t = keep.tile([P, S // STRIPE], U16, name="offs_t")
+        lists = [keep.tile([P, V // STRIPE], U16, name="list%d" % k) for k in range(LISTS)]
         xw = keep.tile([P, T], U32, name="xw", align_bytes=64)
         xs = keep.tile([P, T], U8, name="xs", align_bytes=64)
-        ww_raw = keep.tile([P, 2 * H], U8, name="ww_raw", align_bytes=64)
+        w1w_raw = keep.tile([P, 2 * H], U8, name="w1w_raw", align_bytes=64)
         w3w_raw = keep.tile([P, 2 * N], U8, name="w3w_raw", align_bytes=64)
         ws_raw = keep.tile([P, H], U8, name="ws_raw", align_bytes=64)
-        w2_raw = [keep.tile([P, PACK, H // 2], F32, name="w2_raw%d" % a, align_bytes=64) for a in range(2)]
+        w2_raw = [keep.tile([P, 2, H], F32, name="w2_raw%d" % a, align_bytes=64) for a in range(2)]
         ident = keep.tile([P, P], F32, name="ident", align_bytes=64)
 
-        nc.vector.memset(xs[:, 0 : T // 2].bitcast(I32), 0)
-        nc.gpsimd.memset(xs[:, T // 2 : T].bitcast(I32), 0)
-        nc.gpsimd.memset(ws_raw[:].bitcast(I32), 0)
+        nc.vector.memset(xs[:].bitcast(I32), 0)
+        nc.vector.memset(ws_raw[:].bitcast(I32), 0)
 
         nc.sync.dma_start(offs_t[:], offs)
-        nc.sync.dma_start(out=ww_raw[:].bitcast(I32), in_=w1_words[0].bitcast(I32))
+        nc.sync.dma_start(out=w1w_raw[:].bitcast(I32), in_=w1_words[0].bitcast(I32))
         nc.sync.dma_start(out=w3w_raw[:].bitcast(I32), in_=w3_words[0].bitcast(I32))
-        load_scale_rows([nc.sync] * 4, xs, x_scales[0])
+        load_scale_rows(nc, xs, x_scales[0])
         nc.sync.dma_start(out=xw[:].bitcast(I32), in_=x_words[0].rearrange("p n t -> p (n t)").bitcast(I32))
-        load_scale_rows([nc.sync] * 4, ws_raw, w1_scales[0])
+        load_scale_rows(nc, ws_raw, w1_scales[0])
         nc.sync.dma_start(lists[0][:], p1)
         w2_rows = w2.rearrange("(p j) c -> p j c", j=PACK)
         for a in range(2):
-            nc.sync.dma_start(out=w2_raw[a][:], in_=w2_rows[:, :, a * (H // 2) : (a + 1) * (H // 2)])
+            nc.sync.dma_start(out=w2_raw[a][:], in_=w2_rows[:, 2 * a : 2 * a + 2, :])
         nc.sync.dma_start(lists[1][:], p2)
         nc.sync.dma_start(lists[2][:], p3)
         make_identity(nc, ident[:])
@@ -84,15 +95,16 @@ def tile_picked_aftlocal_none_po_kernel(
         xg_s = keep.tile([P, S], U8, name="xg_s", align_bytes=64)
         xg_w = keep.tile([P, S], U32, name="xg_w", align_bytes=64)
         w1w = keep.tile([P, 2 * H], U8, name="w1w", align_bytes=64)
+        w2_bf = keep.tile([P, PACK, P, PACK], BF16, name="w2_bf", align_bytes=64)
         w1s = keep.tile([P, H], U8, name="w1s", align_bytes=64)
         w3w = keep.tile([P, 2 * N], U8, name="w3w", align_bytes=64)
         w3s = keep.tile([P, N], U8, name="w3s", align_bytes=64)
         nc.vector.tensor_copy(xg_s[:], xs[:].indirect(offs_t[:]))
-        deal_words(nc, w1w, ww_raw)
+        deal_words(nc, w1w, w1w_raw)
         deal_words(nc, w3w, w3w_raw)
         nc.vector.tensor_copy(xg_w[:], xw[:].indirect(offs_t[:]))
         deal_scales(nc, w1s, ws_raw)
-        load_scale_rows([nc.sync] * 4, ws_raw, w3_scales[0])
+        load_scale_rows(nc, ws_raw, w3_scales[0])
 
         def project(bank, codes, scales):
             nc.tensor.matmul_mx(
@@ -106,62 +118,60 @@ def tile_picked_aftlocal_none_po_kernel(
             )
             return bank
 
-        s_banks = [
-            project(in_bank(t, "s_acc"), w1w[:, 256 * t : 256 * (t + 1)].bitcast(FP4X4), w1s[:, P * t : P * (t + 1)])
-            for t in range(PACK)
-        ]
         s_sb = [keep.tile([P, S], F32, name="s%d" % t, align_bytes=64) for t in range(PACK)]
-        nc.scalar.copy(out=s_sb[0][:], in_=s_banks[0][:])
 
-        w2_bf = keep.tile([P, PACK, P, PACK], BF16, name="w2_bf", align_bytes=64)
         w2q = keep.tile([P, H], U32, name="w2q", align_bytes=64)
         w2s = keep.tile([P, H], U8, name="w2s", align_bytes=64)
         for a in range(2):
             nc.vector.tensor_copy(
-                out=w2_bf[:, :, 64 * a : 64 * (a + 1), :].rearrange("p t m j -> p m t j"),
+                out=w2_bf[:, :, :, 2 * a : 2 * a + 2].rearrange("p t m j -> p m t j"),
                 in_=w2_raw[a][:].rearrange("p j (m t) -> p m t j", t=PACK),
             )
         for t in range(PACK):
             nc.vector.quantize_mx(
-                out=w2q[:, P * t : P * (t + 1)].bitcast(FP8X4),
-                scales=w2s[:, P * t : P * (t + 1)],
+                out=w2q[:, tile_cols(t)].bitcast(FP8X4),
+                scales=w2s[:, tile_cols(t)],
                 in_=w2_bf[:, t, :, :].rearrange("p m j -> p (m j)"),
             )
 
-        val_banks = [
-            project(in_bank(4 + t, "val_acc"), w2q[:, P * t : P * (t + 1)].bitcast(FP8X4), w2s[:, P * t : P * (t + 1)])
-            for t in range(PACK)
-        ]
+        s_banks, val_banks = [], []
+        for t in range(PACK):
+            w1_codes = w1w[:, tile_cols(t, 2 * P)].bitcast(FP4X4)
+            s_banks.append(project(in_bank(S_BANKS[t], "s_acc"), w1_codes, w1s[:, tile_cols(t)]))
+            w2_codes = w2q[:, tile_cols(t)].bitcast(FP8X4)
+            val_banks.append(project(in_bank(VAL_BANKS[t], "val_acc"), w2_codes, w2s[:, tile_cols(t)]))
+        nc.scalar.copy(out=s_sb[0][:], in_=s_banks[0][:])
 
         def add_turned(acc, terms):
-            for k in range(3):
-                nc.tensor.matmul(acc, terms[k], ident[:], start=(k == 0), stop=(k == 2), is_transpose=True)
+            for k in range(LISTS):
+                nc.tensor.matmul(acc, terms[k], ident[:], start=(k == 0), stop=(k == LISTS - 1), is_transpose=True)
 
-        den = [in_bank(h, "den") for h in range(HALVES)]
-        num = [in_bank(2 + h, "num") for h in range(HALVES)]
+        den = [in_bank(DEN_BANKS[h], "den") for h in range(HALVES)]
+        num = [in_bank(NUM_BANKS[h], "num") for h in range(HALVES)]
         for t in range(PACK):
-            e = [keep.tile([P, V], F32, name="e%d_%d" % (t, k), align_bytes=64) for k in range(3)]
-            ev = [keep.tile([P, V], F32, name="ev%d_%d" % (t, k), align_bytes=64) for k in range(3)]
-            for k in range(3):
+            last = t == PACK - 1
+            e = [keep.tile([P, V], F32, name="e%d_%d" % (t, k), align_bytes=64) for k in range(LISTS)]
+            ev = [keep.tile([P, V], F32, name="ev%d_%d" % (t, k), align_bytes=64) for k in range(LISTS)]
+            for k in range(LISTS):
                 nc.scalar.activation(e[k][:], s_sb[t][:].indirect(lists[k][:]), ACT.Exp)
-            if t + 1 < PACK:
+            if not last:
                 nc.scalar.copy(out=s_sb[t + 1][:], in_=s_banks[t + 1][:])
             val_t = keep.tile([P, S], F32, name="val%d" % t, align_bytes=64)
             nc.vector.tensor_copy(out=val_t[:], in_=val_banks[t][:])
             for h in range(HALVES):
-                add_turned(den[h][:, P * t : P * (t + 1)], [e[k][:, VH * h : VH * (h + 1)] for k in range(3)])
-            if t + 1 < PACK:
-                for k in range(3):
+                add_turned(den[h][:, tile_cols(t)], [e[k][:, tile_cols(h)] for k in range(LISTS)])
+            if not last:
+                for k in range(LISTS):
                     nc.vector.tensor_tensor(ev[k][:], val_t[:].indirect(lists[k][:]), e[k][:], MULT)
                 for h in range(HALVES):
-                    add_turned(num[h][:, P * t : P * (t + 1)], [ev[k][:, VH * h : VH * (h + 1)] for k in range(3)])
+                    add_turned(num[h][:, tile_cols(t)], [ev[k][:, tile_cols(h)] for k in range(LISTS)])
             else:
                 for h in range(HALVES):
-                    cols = slice(VH * h, VH * (h + 1))
-                    for k in range(3):
-                        offsets = lists[k][:, VH // 16 * h : VH // 16 * (h + 1)]
-                        nc.vector.tensor_tensor(ev[k][:, cols], val_t[:].indirect(offsets), e[k][:, cols], MULT)
-                    add_turned(num[h][:, P * t : P * (t + 1)], [ev[k][:, cols] for k in range(3)])
+                    places = tile_cols(h)
+                    for k in range(LISTS):
+                        offsets = lists[k][:, tile_cols(h, P // STRIPE)]
+                        nc.vector.tensor_tensor(ev[k][:, places], val_t[:].indirect(offsets), e[k][:, places], MULT)
+                    add_turned(num[h][:, tile_cols(t)], [ev[k][:, places] for k in range(LISTS)])
 
         deal_scales(nc, w3s, ws_raw)
 
@@ -170,61 +180,63 @@ def tile_picked_aftlocal_none_po_kernel(
         out_rows = out_0.rearrange("(p t) v -> p t v", t=PACK)
         out_words = out_1[0].rearrange("p v r -> p (v r)").bitcast(I32)
         for h in range(HALVES):
-            cols = slice(VH * h, VH * (h + 1))
+            places = tile_cols(h)
             root = keep.tile([P, H], F32, name="root%d" % h, align_bytes=64)
             inv = keep.tile([P, H], F32, name="inv%d" % h, align_bytes=64)
             nc.scalar.activation(
-                root[:].rearrange("v (u p e) -> v u p e", u=2, e=2),
-                den[h][:].rearrange("v (u e p) -> v u p e", u=2, e=2),
+                root[:].rearrange("v (u p d) -> v u p d", u=2, d=2),
+                den[h][:].rearrange("v (u d p) -> v u p d", u=2, d=2),
                 ACT.Abs_reciprocal_sqrt,
             )
-            nc.scalar.activation(inv[:], root[:], ACT.Square)
-            z_t = keep.tile([P, H], BF16, name="z_t%d" % h, align_bytes=64)
-            nc.vector.tensor_tensor(
-                z_t[:].rearrange("v (u p e) -> v u p e", u=2, e=2),
-                num[h][:].rearrange("v (u e p) -> v u p e", u=2, e=2),
-                inv[:].rearrange("v (u p e) -> v u p e", u=2, e=2),
-                MULT,
-            )
-            turned = in_bank(4 + h, "turned")
-            z_pairs = z_t[:].bitcast(F32)
+            z_turned = keep.tile([P, H], BF16, name="z_turned%d" % h, align_bytes=64)
+            z_pairs = in_bank(TURN_BANKS[h], "z_pairs")
             for u in range(2):
-                nc.tensor.transpose(turned[:, P * u : P * (u + 1)], z_pairs[:, P * u : P * (u + 1)], ident[:])
-            z_bf = keep.tile([P, VH * PACK], BF16, name="z_bf%d" % h, align_bytes=64)
+                pair = tile_cols(u, 2 * P)
+                nc.scalar.activation(inv[:, pair], root[:, pair], ACT.Square)
+                nc.vector.tensor_tensor(
+                    z_turned[:, pair].rearrange("v (p d) -> v p d", d=2),
+                    num[h][:, pair].rearrange("v (d p) -> v p d", d=2),
+                    inv[:, pair].rearrange("v (p d) -> v p d", d=2),
+                    MULT,
+                )
+                nc.tensor.transpose(z_pairs[:, tile_cols(u)], z_turned[:, pair].bitcast(F32), ident[:])
+            z_bf = keep.tile([P, P * PACK], BF16, name="z_bf%d" % h, align_bytes=64)
             nc.scalar.copy(
                 out=z_bf[:].bitcast(F32).rearrange("p (v u) -> p v u", u=2),
-                in_=turned[:, 0 : 2 * P].rearrange("p (u v) -> p v u", u=2),
+                in_=z_pairs[:, 0 : 2 * P].rearrange("p (u v) -> p v u", u=2),
             )
-            zq = keep.tile([P, VH], U32, name="zq%d" % h, align_bytes=64)
-            zs = keep.tile([P, VH], U8, name="zs%d" % h, align_bytes=64)
+            zq = keep.tile([P, P], U32, name="zq%d" % h, align_bytes=64)
+            zs = keep.tile([P, P], U8, name="zs%d" % h, align_bytes=64)
             nc.vector.quantize_mx(out=zq[:].bitcast(FP8X4), scales=zs[:], in_=z_bf[:])
-            y = keep.tile([P, PACK, VH], F32, name="y%d" % h, align_bytes=64)
-            for u in range(2):
-                bank = in_bank((6 + 2 * h + u) % 8, "y_acc")
-                for t in range(2 * u, 2 * u + 2):
+
+            y = keep.tile([P, PACK, P], F32, name="y%d" % h, align_bytes=64)
+            for u, copy in enumerate((nc.scalar.copy, nc.vector.tensor_copy)):
+                y_acc = in_bank(Y_BANKS[h][u], "y_acc")
+                for d in range(2):
+                    t = 2 * u + d
                     nc.tensor.matmul_mx(
-                        out=bank[:, VH * (t % 2) : VH * (t % 2 + 1)],
-                        lhsT=w3w[:, 256 * t : 256 * (t + 1)].bitcast(FP4X4),
-                        lhsT_scale=w3s[:, P * t : P * (t + 1)],
+                        out=y_acc[:, tile_cols(d)],
+                        lhsT=w3w[:, tile_cols(t, 2 * P)].bitcast(FP4X4),
+                        lhsT_scale=w3s[:, tile_cols(t)],
                         rhs=zq[:].bitcast(FP8X4),
                         rhs_scale=zs[:],
                         start=True,
                         stop=True,
                     )
-                y_pair = y[:, 2 * u : 2 * u + 2, :].rearrange("p t v -> p (t v)")
-                if u == 0:
-                    nc.scalar.copy(out=y_pair, in_=bank[:, 0 : 2 * VH])
-                else:
-                    nc.vector.tensor_copy(out=y_pair, in_=bank[:, 0 : 2 * VH])
-            nc.sync.dma_start(out=out_rows[:, :, cols], in_=y[:])
-            y_bf = keep.tile([P, VH, PACK], BF16, name="y_bf%d" % h, align_bytes=64)
+                copy(out=y[:, 2 * u : 2 * u + 2, :].rearrange("p t v -> p (t v)"), in_=y_acc[:, 0 : 2 * P])
+            nc.sync.dma_start(out=out_rows[:, :, places], in_=y[:])
+
+            y_bf = keep.tile([P, P, PACK], BF16, name="y_bf%d" % h, align_bytes=64)
             nc.vector.tensor_copy(out=y_bf[:], in_=y[:].rearrange("p t v -> p v t"))
             nc.vector.quantize_mx(
-                out=y_words[:, cols].bitcast(FP8X4), scales=y_scales[:, cols], in_=y_bf[:].rearrange("p v t -> p (v t)")
+                out=y_words[:, places].bitcast(FP8X4),
+                scales=y_scales[:, places],
+                in_=y_bf[:].rearrange("p v t -> p (v t)"),
             )
-            nc.sync.dma_start(out=out_words[:, cols], in_=y_words[:, cols].bitcast(I32))
-        for q in range(4):
-            queue = nc.sync if q % 2 == 0 else nc.scalar
+            nc.sync.dma_start(out=out_words[:, places], in_=y_words[:, places].bitcast(I32))
+
+        for q in range(QUADRANTS):
+            queue = (nc.sync, nc.scalar)[q % 2]
             queue.dma_start(
                 out=out_2[0][4 * q : 4 * q + 4, :].bitcast(I32), in_=y_scales[32 * q : 32 * q + 4, :].bitcast(I32)
             )

@@ -32,9 +32,9 @@ TURN_BANKS = (2, 3)
 Y_BANKS = ((6, 7), (4, 5))
 
 
-def load_scale_rows(nc, plane, rows):
-    for q in range(QUADRANTS):
-        nc.sync.dma_start(out=plane[32 * q : 32 * q + 4, :].bitcast(I32), in_=rows[4 * q : 4 * q + 4, :].bitcast(I32))
+def load_scale_rows(queues, plane, rows):
+    for r in range(4):
+        queues[r % len(queues)].dma_start(out=plane[r:P:32, :].bitcast(I32), in_=rows[r:16:4, :].bitcast(I32))
 
 
 def deal_words(nc, dealt, raw):
@@ -48,6 +48,13 @@ def deal_scales(nc, dealt, raw):
     nc.vector.tensor_copy(
         out=dealt[:].rearrange("p (t a m) -> p a t m", t=PACK, m=16),
         in_=raw[:].rearrange("p (a m t) -> p a t m", t=PACK, m=16),
+    )
+
+
+def deal_fours(nc, dealt, raw):
+    nc.vector.tensor_copy(
+        out=dealt[:].bitcast(I32).rearrange("p (t a q w) -> p a t q w", t=PACK, a=8, q=4),
+        in_=raw[:].bitcast(I32).rearrange("p (a q t w) -> p a t q w", t=PACK, a=8, q=4),
     )
 
 
@@ -72,18 +79,20 @@ def tile_picked_aftlocal_none_po_kernel(
         w1w_raw = keep.tile([P, 2 * H], U8, name="w1w_raw", align_bytes=64)
         w3w_raw = keep.tile([P, 2 * N], U8, name="w3w_raw", align_bytes=64)
         ws_raw = keep.tile([P, H], U8, name="ws_raw", align_bytes=64)
-        w2_raw = [keep.tile([P, 2, H], F32, name="w2_raw%d" % a, align_bytes=64) for a in range(2)]
+        w2_raw = [keep.tile([P, 2, H], F32, name="w2_raw%d" % a, tag="w2_raw%d" % a, align_bytes=64) for a in range(2)]
         ident = keep.tile([P, P], F32, name="ident", align_bytes=64)
 
-        nc.vector.memset(xs[:].bitcast(I32), 0)
+        nc.gpsimd.memset(xs[:, : T // 2].bitcast(I32), 0)
+        nc.vector.memset(xs[:, T // 2 :].bitcast(I32), 0)
         nc.vector.memset(ws_raw[:].bitcast(I32), 0)
 
         nc.sync.dma_start(offs_t[:], offs)
         nc.sync.dma_start(out=w1w_raw[:].bitcast(I32), in_=w1_words[0].bitcast(I32))
         nc.sync.dma_start(out=w3w_raw[:].bitcast(I32), in_=w3_words[0].bitcast(I32))
-        load_scale_rows(nc, xs, x_scales[0])
-        nc.sync.dma_start(out=xw[:].bitcast(I32), in_=x_words[0].rearrange("p n t -> p (n t)").bitcast(I32))
-        load_scale_rows(nc, ws_raw, w1_scales[0])
+        x_rows = x_words[0].rearrange("p n t -> p (n t)").bitcast(I32)
+        load_scale_rows((nc.sync,), xs, x_scales[0])
+        nc.sync.dma_start(out=xw[:].bitcast(I32), in_=x_rows)
+        load_scale_rows((nc.sync,), ws_raw, w1_scales[0])
         nc.sync.dma_start(lists[0][:], p1)
         w2_rows = w2.rearrange("(p j) c -> p j c", j=PACK)
         for a in range(2):
@@ -95,16 +104,15 @@ def tile_picked_aftlocal_none_po_kernel(
         xg_s = keep.tile([P, S], U8, name="xg_s", align_bytes=64)
         xg_w = keep.tile([P, S], U32, name="xg_w", align_bytes=64)
         w1w = keep.tile([P, 2 * H], U8, name="w1w", align_bytes=64)
-        w2_bf = keep.tile([P, PACK, P, PACK], BF16, name="w2_bf", align_bytes=64)
+        w2_bf = keep.tile([P, PACK, P, PACK], BF16, name="w2_bf", tag="w2_bf", align_bytes=64)
         w1s = keep.tile([P, H], U8, name="w1s", align_bytes=64)
         w3w = keep.tile([P, 2 * N], U8, name="w3w", align_bytes=64)
-        w3s = keep.tile([P, N], U8, name="w3s", align_bytes=64)
         nc.vector.tensor_copy(xg_s[:], xs[:].indirect(offs_t[:]))
-        deal_words(nc, w1w, w1w_raw)
+        deal_fours(nc, w1w, w1w_raw)
         deal_words(nc, w3w, w3w_raw)
         nc.vector.tensor_copy(xg_w[:], xw[:].indirect(offs_t[:]))
-        deal_scales(nc, w1s, ws_raw)
-        load_scale_rows(nc, ws_raw, w3_scales[0])
+        deal_fours(nc, w1s, ws_raw)
+        load_scale_rows((nc.sync,), ws_raw, w3_scales[0])
 
         def project(bank, codes, scales):
             nc.tensor.matmul_mx(
@@ -122,17 +130,25 @@ def tile_picked_aftlocal_none_po_kernel(
 
         w2q = keep.tile([P, H], U32, name="w2q", align_bytes=64)
         w2s = keep.tile([P, H], U8, name="w2s", align_bytes=64)
-        for a in range(2):
+
+        def round_w2(a, tiles):
             nc.vector.tensor_copy(
-                out=w2_bf[:, :, :, 2 * a : 2 * a + 2].rearrange("p t m j -> p m t j"),
-                in_=w2_raw[a][:].rearrange("p j (m t) -> p m t j", t=PACK),
+                out=w2_bf[:, tiles, :, 2 * a : 2 * a + 2].rearrange("p t (q c) j -> p t q c j", c=PACK),
+                in_=w2_raw[a][:].rearrange("p j (q t c) -> p t q c j", t=PACK, c=PACK)[:, tiles],
             )
-        for t in range(PACK):
+
+        def quantize_w2(t):
             nc.vector.quantize_mx(
                 out=w2q[:, tile_cols(t)].bitcast(FP8X4),
                 scales=w2s[:, tile_cols(t)],
                 in_=w2_bf[:, t, :, :].rearrange("p m j -> p (m j)"),
             )
+
+        round_w2(0, slice(0, PACK))
+        round_w2(1, slice(0, 2))
+        round_w2(1, slice(2, PACK))
+        for t in range(PACK):
+            quantize_w2(t)
 
         s_banks, val_banks = [], []
         for t in range(PACK):
@@ -173,6 +189,7 @@ def tile_picked_aftlocal_none_po_kernel(
                         nc.vector.tensor_tensor(ev[k][:, places], val_t[:].indirect(offsets), e[k][:, places], MULT)
                     add_turned(num[h][:, tile_cols(t)], [ev[k][:, places] for k in range(LISTS)])
 
+        w3s = keep.tile([P, N], U8, name="w3s", tag="w2_raw1", align_bytes=64)
         deal_scales(nc, w3s, ws_raw)
 
         y_words = keep.tile([P, V], U32, name="y_words", align_bytes=64)
@@ -183,20 +200,20 @@ def tile_picked_aftlocal_none_po_kernel(
             places = tile_cols(h)
             root = keep.tile([P, H], F32, name="root%d" % h, align_bytes=64)
             inv = keep.tile([P, H], F32, name="inv%d" % h, align_bytes=64)
-            nc.scalar.activation(
-                root[:].rearrange("v (u p d) -> v u p d", u=2, d=2),
-                den[h][:].rearrange("v (u d p) -> v u p d", u=2, d=2),
-                ACT.Abs_reciprocal_sqrt,
-            )
             z_turned = keep.tile([P, H], BF16, name="z_turned%d" % h, align_bytes=64)
             z_pairs = in_bank(TURN_BANKS[h], "z_pairs")
             for u in range(2):
                 pair = tile_cols(u, 2 * P)
+                nc.scalar.activation(
+                    root[:, pair].rearrange("v (q t d) -> v q t d", t=PACK, d=2),
+                    den[h][:].rearrange("v (t q u d) -> v u q t d", t=PACK, u=2, d=2)[:, u],
+                    ACT.Abs_reciprocal_sqrt,
+                )
                 nc.scalar.activation(inv[:, pair], root[:, pair], ACT.Square)
                 nc.vector.tensor_tensor(
-                    z_turned[:, pair].rearrange("v (p d) -> v p d", d=2),
-                    num[h][:, pair].rearrange("v (d p) -> v p d", d=2),
-                    inv[:, pair].rearrange("v (p d) -> v p d", d=2),
+                    z_turned[:, pair].rearrange("v (q t d) -> v q t d", t=PACK, d=2),
+                    num[h][:].rearrange("v (t q u d) -> v u q t d", t=PACK, u=2, d=2)[:, u],
+                    inv[:, pair].rearrange("v (q t d) -> v q t d", t=PACK, d=2),
                     MULT,
                 )
                 nc.tensor.transpose(z_pairs[:, tile_cols(u)], z_turned[:, pair].bitcast(F32), ident[:])

@@ -29,6 +29,7 @@ VAL_BANKS = (4, 5, 6, 7)
 DEN_BANKS = (4, 5)
 NUM_BANKS = (0, 1)
 TURN_BANKS = (2, 3)
+TWIN_BANK = 0
 Y_BANKS = ((6, 7), (4, 5))
 
 
@@ -79,7 +80,8 @@ def tile_picked_aftlocal_none_po_kernel(
         w1w_raw = keep.tile([P, 2 * H], U8, name="w1w_raw", align_bytes=64)
         w3w_raw = keep.tile([P, 2 * N], U8, name="w3w_raw", align_bytes=64)
         ws_raw = keep.tile([P, H], U8, name="ws_raw", align_bytes=64)
-        w2_raw = [keep.tile([P, 2, H], F32, name="w2_raw%d" % a, tag="w2_raw%d" % a, align_bytes=64) for a in range(2)]
+        w2_lo = keep.tile([P, 2, H], F32, name="w2_lo", align_bytes=64)
+        w2_hi = [keep.tile([P, 2, H // 2], F32, name="w2_hi%d" % b, tag="w2_hi%d" % b, align_bytes=64) for b in range(2)]
         ident = keep.tile([P, P], F32, name="ident", align_bytes=64)
 
         nc.gpsimd.memset(xs[:, : T // 2].bitcast(I32), 0)
@@ -92,11 +94,12 @@ def tile_picked_aftlocal_none_po_kernel(
         x_rows = x_words[0].rearrange("p n t -> p (n t)").bitcast(I32)
         load_scale_rows((nc.sync,), xs, x_scales[0])
         nc.sync.dma_start(out=xw[:].bitcast(I32), in_=x_rows)
-        load_scale_rows((nc.sync,), ws_raw, w1_scales[0])
         nc.sync.dma_start(lists[0][:], p1)
+        load_scale_rows((nc.sync,), ws_raw, w1_scales[0])
         w2_rows = w2.rearrange("(p j) c -> p j c", j=PACK)
-        for a in range(2):
-            nc.sync.dma_start(out=w2_raw[a][:], in_=w2_rows[:, 2 * a : 2 * a + 2, :])
+        nc.sync.dma_start(out=w2_lo[:], in_=w2_rows[:, 0:2, :])
+        for b in range(2):
+            nc.sync.dma_start(out=w2_hi[b][:], in_=w2_rows[:, 2:4, tile_cols(b, H // 2)])
         nc.sync.dma_start(lists[1][:], p2)
         nc.sync.dma_start(lists[2][:], p3)
         make_identity(nc, ident[:])
@@ -131,10 +134,10 @@ def tile_picked_aftlocal_none_po_kernel(
         w2q = keep.tile([P, H], U32, name="w2q", align_bytes=64)
         w2s = keep.tile([P, H], U8, name="w2s", align_bytes=64)
 
-        def round_w2(a, tiles):
+        def round_w2(raw, rows, places, tiles=slice(0, PACK)):
             nc.vector.tensor_copy(
-                out=w2_bf[:, tiles, :, 2 * a : 2 * a + 2].rearrange("p t (q c) j -> p t q c j", c=PACK),
-                in_=w2_raw[a][:].rearrange("p j (q t c) -> p t q c j", t=PACK, c=PACK)[:, tiles],
+                out=w2_bf[:, tiles, places, rows].rearrange("p t (q c) j -> p t q c j", c=PACK),
+                in_=raw[:].rearrange("p j (q t c) -> p t q c j", t=PACK, c=PACK)[:, tiles],
             )
 
         def quantize_w2(t):
@@ -144,9 +147,10 @@ def tile_picked_aftlocal_none_po_kernel(
                 in_=w2_bf[:, t, :, :].rearrange("p m j -> p (m j)"),
             )
 
-        round_w2(0, slice(0, PACK))
-        round_w2(1, slice(0, 2))
-        round_w2(1, slice(2, PACK))
+        round_w2(w2_lo, slice(0, 2), slice(0, P))
+        round_w2(w2_hi[0], slice(2, 4), tile_cols(0, P // 2))
+        round_w2(w2_hi[1], slice(2, 4), tile_cols(1, P // 2), slice(0, 2))
+        round_w2(w2_hi[1], slice(2, 4), tile_cols(1, P // 2), slice(2, PACK))
         for t in range(PACK):
             quantize_w2(t)
 
@@ -189,19 +193,18 @@ def tile_picked_aftlocal_none_po_kernel(
                         nc.vector.tensor_tensor(ev[k][:, places], val_t[:].indirect(offsets), e[k][:, places], MULT)
                     add_turned(num[h][:, tile_cols(t)], [ev[k][:, places] for k in range(LISTS)])
 
-        w3s = keep.tile([P, N], U8, name="w3s", tag="w2_raw1", align_bytes=64)
+        w3s = keep.tile([P, N], U8, name="w3s", tag="w2_hi1", align_bytes=64)
         deal_scales(nc, w3s, ws_raw)
 
         y_words = keep.tile([P, V], U32, name="y_words", align_bytes=64)
         y_scales = keep.tile([P, V], U8, name="y_scales", align_bytes=64)
         out_rows = out_0.rearrange("(p t) v -> p t v", t=PACK)
         out_words = out_1[0].rearrange("p v r -> p (v r)").bitcast(I32)
+        factor = []
         for h in range(HALVES):
-            places = tile_cols(h)
             root = keep.tile([P, H], F32, name="root%d" % h, align_bytes=64)
-            inv = keep.tile([P, H], F32, name="inv%d" % h, align_bytes=64)
-            z_turned = keep.tile([P, H], BF16, name="z_turned%d" % h, align_bytes=64)
-            z_pairs = in_bank(TURN_BANKS[h], "z_pairs")
+            other = keep.tile([P, H], F32, name="other%d" % h, align_bytes=64)
+            factor.append((root, other))
             for u in range(2):
                 pair = tile_cols(u, 2 * P)
                 nc.scalar.activation(
@@ -209,13 +212,31 @@ def tile_picked_aftlocal_none_po_kernel(
                     den[h][:].rearrange("v (t q u d) -> v u q t d", t=PACK, u=2, d=2)[:, u],
                     ACT.Abs_reciprocal_sqrt,
                 )
-                nc.scalar.activation(inv[:, pair], root[:, pair], ACT.Square)
-                nc.vector.tensor_tensor(
-                    z_turned[:, pair].rearrange("v (q t d) -> v q t d", t=PACK, d=2),
-                    num[h][:].rearrange("v (t q u d) -> v u q t d", t=PACK, u=2, d=2)[:, u],
-                    inv[:, pair].rearrange("v (q t d) -> v q t d", t=PACK, d=2),
-                    MULT,
-                )
+                if h == 0:
+                    nc.vector.tensor_tensor(
+                        other[:, pair].rearrange("v (q t d) -> v q t d", t=PACK, d=2),
+                        num[h][:].rearrange("v (t q u d) -> v u q t d", t=PACK, u=2, d=2)[:, u],
+                        root[:, pair].rearrange("v (q t d) -> v q t d", t=PACK, d=2),
+                        MULT,
+                    )
+                else:
+                    nc.scalar.activation(other[:, pair], root[:, pair], ACT.Square)
+        for h in range(HALVES):
+            places = tile_cols(h)
+            z_turned = keep.tile([P, H], BF16, name="z_turned%d" % h, align_bytes=64)
+            z_pairs = in_bank(TURN_BANKS[h], "z_pairs")
+            for u in range(2):
+                pair = tile_cols(u, 2 * P)
+                root, other = factor[h]
+                if h == 0:
+                    nc.vector.tensor_tensor(z_turned[:, pair], other[:, pair], root[:, pair], MULT)
+                else:
+                    nc.vector.tensor_tensor(
+                        z_turned[:, pair].rearrange("v (q t d) -> v q t d", t=PACK, d=2),
+                        num[h][:].rearrange("v (t q u d) -> v u q t d", t=PACK, u=2, d=2)[:, u],
+                        other[:, pair].rearrange("v (q t d) -> v q t d", t=PACK, d=2),
+                        MULT,
+                    )
                 nc.tensor.transpose(z_pairs[:, tile_cols(u)], z_turned[:, pair].bitcast(F32), ident[:])
             z_bf = keep.tile([P, P * PACK], BF16, name="z_bf%d" % h, align_bytes=64)
             nc.scalar.copy(
@@ -227,24 +248,33 @@ def tile_picked_aftlocal_none_po_kernel(
             nc.vector.quantize_mx(out=zq[:].bitcast(FP8X4), scales=zs[:], in_=z_bf[:])
 
             y = keep.tile([P, PACK, P], F32, name="y%d" % h, align_bytes=64)
-            for u, copy in enumerate((nc.scalar.copy, nc.vector.tensor_copy)):
+            y_bf = keep.tile([P, P, PACK], BF16, name="y_bf%d" % h, align_bytes=64)
+
+            def last_layer(acc, t):
+                nc.tensor.matmul_mx(
+                    out=acc,
+                    lhsT=w3w[:, tile_cols(t, 2 * P)].bitcast(FP4X4),
+                    lhsT_scale=w3s[:, tile_cols(t)],
+                    rhs=zq[:].bitcast(FP8X4),
+                    rhs_scale=zs[:],
+                    start=True,
+                    stop=True,
+                )
+
+            if h == HALVES - 1:
+                twin = in_bank(TWIN_BANK, "y_twin")
+                for t in range(PACK):
+                    last_layer(twin[:, tile_cols(t)], t)
+                nc.vector.tensor_copy(out=y_bf[:], in_=twin[:].rearrange("p (t v) -> p v t", t=PACK))
+            for u in range(2):
                 y_acc = in_bank(Y_BANKS[h][u], "y_acc")
                 for d in range(2):
-                    t = 2 * u + d
-                    nc.tensor.matmul_mx(
-                        out=y_acc[:, tile_cols(d)],
-                        lhsT=w3w[:, tile_cols(t, 2 * P)].bitcast(FP4X4),
-                        lhsT_scale=w3s[:, tile_cols(t)],
-                        rhs=zq[:].bitcast(FP8X4),
-                        rhs_scale=zs[:],
-                        start=True,
-                        stop=True,
-                    )
-                copy(out=y[:, 2 * u : 2 * u + 2, :].rearrange("p t v -> p (t v)"), in_=y_acc[:, 0 : 2 * P])
+                    last_layer(y_acc[:, tile_cols(d)], 2 * u + d)
+                nc.scalar.copy(out=y[:, 2 * u : 2 * u + 2, :].rearrange("p t v -> p (t v)"), in_=y_acc[:, 0 : 2 * P])
             nc.sync.dma_start(out=out_rows[:, :, places], in_=y[:])
 
-            y_bf = keep.tile([P, P, PACK], BF16, name="y_bf%d" % h, align_bytes=64)
-            nc.vector.tensor_copy(out=y_bf[:], in_=y[:].rearrange("p t v -> p v t"))
+            if h < HALVES - 1:
+                nc.vector.tensor_copy(out=y_bf[:], in_=y[:].rearrange("p t v -> p v t"))
             nc.vector.quantize_mx(
                 out=y_words[:, places].bitcast(FP8X4),
                 scales=y_scales[:, places],

@@ -52,10 +52,10 @@ def deal_scales(nc, dealt, raw):
     )
 
 
-def deal_fours(nc, dealt, raw):
+def deal_fours(nc, dealt, raw, tiles=slice(0, PACK)):
     nc.vector.tensor_copy(
-        out=dealt[:].bitcast(I32).rearrange("p (t a q w) -> p a t q w", t=PACK, a=8, q=4),
-        in_=raw[:].bitcast(I32).rearrange("p (a q t w) -> p a t q w", t=PACK, a=8, q=4),
+        out=dealt[:].bitcast(I32).rearrange("p (t a q w) -> p a t q w", t=tiles.stop - tiles.start, a=8, q=4),
+        in_=raw[:].bitcast(I32).rearrange("p (a q t w) -> p a t q w", t=PACK, a=8, q=4)[:, :, tiles],
     )
 
 
@@ -79,14 +79,16 @@ def tile_picked_aftlocal_none_po_kernel(
         xs = keep.tile([P, T], U8, name="xs", align_bytes=64)
         w1w_raw = keep.tile([P, 2 * H], U8, name="w1w_raw", align_bytes=64)
         w3w_raw = keep.tile([P, 2 * N], U8, name="w3w_raw", align_bytes=64)
-        ws_raw = keep.tile([P, H], U8, name="ws_raw", align_bytes=64)
+        w1s_raw = keep.tile([P, H], U8, name="w1s_raw", align_bytes=64)
+        w3s_raw = keep.tile([P, N], U8, name="w3s_raw", align_bytes=64)
         w2_lo = keep.tile([P, 2, H], F32, name="w2_lo", align_bytes=64)
         w2_hi = [keep.tile([P, 2, H // 2], F32, name="w2_hi%d" % b, tag="w2_hi%d" % b, align_bytes=64) for b in range(2)]
         ident = keep.tile([P, P], F32, name="ident", align_bytes=64)
 
         nc.gpsimd.memset(xs[:, : T // 2].bitcast(I32), 0)
         nc.vector.memset(xs[:, T // 2 :].bitcast(I32), 0)
-        nc.vector.memset(ws_raw[:].bitcast(I32), 0)
+        nc.vector.memset(w1s_raw[:].bitcast(I32), 0)
+        nc.vector.memset(w3s_raw[:].bitcast(I32), 0)
 
         nc.sync.dma_start(offs_t[:], offs)
         nc.sync.dma_start(out=w1w_raw[:].bitcast(I32), in_=w1_words[0].bitcast(I32))
@@ -95,27 +97,27 @@ def tile_picked_aftlocal_none_po_kernel(
         load_scale_rows((nc.sync,), xs, x_scales[0])
         nc.sync.dma_start(out=xw[:].bitcast(I32), in_=x_rows)
         nc.sync.dma_start(lists[0][:], p1)
-        load_scale_rows((nc.sync,), ws_raw, w1_scales[0])
+        load_scale_rows((nc.sync,), w1s_raw, w1_scales[0])
         w2_rows = w2.rearrange("(p j) c -> p j c", j=PACK)
         nc.sync.dma_start(out=w2_lo[:], in_=w2_rows[:, 0:2, :])
         for b in range(2):
             nc.sync.dma_start(out=w2_hi[b][:], in_=w2_rows[:, 2:4, tile_cols(b, H // 2)])
         nc.sync.dma_start(lists[1][:], p2)
         nc.sync.dma_start(lists[2][:], p3)
+        load_scale_rows((nc.sync,), w3s_raw, w3_scales[0])
         make_identity(nc, ident[:])
 
         xg_s = keep.tile([P, S], U8, name="xg_s", align_bytes=64)
         xg_w = keep.tile([P, S], U32, name="xg_w", align_bytes=64)
         w1w = keep.tile([P, 2 * H], U8, name="w1w", align_bytes=64)
         w2_bf = keep.tile([P, PACK, P, PACK], BF16, name="w2_bf", tag="w2_bf", align_bytes=64)
-        w1s = keep.tile([P, H], U8, name="w1s", align_bytes=64)
+        w1s = [keep.tile([P, H // 2], U8, name="w1s0", align_bytes=64)]
         w3w = keep.tile([P, 2 * N], U8, name="w3w", align_bytes=64)
         nc.vector.tensor_copy(xg_s[:], xs[:].indirect(offs_t[:]))
         deal_fours(nc, w1w, w1w_raw)
         deal_words(nc, w3w, w3w_raw)
         nc.vector.tensor_copy(xg_w[:], xw[:].indirect(offs_t[:]))
-        deal_fours(nc, w1s, ws_raw)
-        load_scale_rows((nc.sync,), ws_raw, w3_scales[0])
+        deal_fours(nc, w1s[0], w1s_raw, slice(0, 2))
 
         def project(bank, codes, scales):
             nc.tensor.matmul_mx(
@@ -153,11 +155,13 @@ def tile_picked_aftlocal_none_po_kernel(
         round_w2(w2_hi[1], slice(2, 4), tile_cols(1, P // 2), slice(2, PACK))
         for t in range(PACK):
             quantize_w2(t)
+        w1s.append(keep.tile([P, H // 2], U8, name="w1s1", tag="w2_bf", align_bytes=64))
+        deal_fours(nc, w1s[1], w1s_raw, slice(2, PACK))
 
         s_banks, val_banks = [], []
         for t in range(PACK):
             w1_codes = w1w[:, tile_cols(t, 2 * P)].bitcast(FP4X4)
-            s_banks.append(project(in_bank(S_BANKS[t], "s_acc"), w1_codes, w1s[:, tile_cols(t)]))
+            s_banks.append(project(in_bank(S_BANKS[t], "s_acc"), w1_codes, w1s[t // 2][:, tile_cols(t % 2)]))
             w2_codes = w2q[:, tile_cols(t)].bitcast(FP8X4)
             val_banks.append(project(in_bank(VAL_BANKS[t], "val_acc"), w2_codes, w2s[:, tile_cols(t)]))
         nc.scalar.copy(out=s_sb[0][:], in_=s_banks[0][:])
@@ -194,7 +198,7 @@ def tile_picked_aftlocal_none_po_kernel(
                     add_turned(num[h][:, tile_cols(t)], [ev[k][:, places] for k in range(LISTS)])
 
         w3s = keep.tile([P, N], U8, name="w3s", tag="w2_hi1", align_bytes=64)
-        deal_scales(nc, w3s, ws_raw)
+        deal_scales(nc, w3s, w3s_raw)
 
         y_words = keep.tile([P, V], U32, name="y_words", align_bytes=64)
         y_scales = keep.tile([P, V], U8, name="y_scales", align_bytes=64)

@@ -23,19 +23,19 @@ LISTS = 3
 QUADRANTS = 4
 STRIPE = 16
 HALVES = V // P
+PAIRS = 2
 
 S_BANKS = (0, 1, 2, 3)
 VAL_BANKS = (4, 5, 6, 7)
 DEN_BANKS = (4, 5)
 NUM_BANKS = (0, 1)
 TURN_BANKS = (2, 3)
-TWIN_BANK = 0
 Y_BANKS = ((6, 7), (4, 5))
 
 
-def load_scale_rows(queues, plane, rows):
-    for r in range(4):
-        queues[r % len(queues)].dma_start(out=plane[r:P:32, :].bitcast(I32), in_=rows[r:16:4, :].bitcast(I32))
+def load_scale_rows(nc, plane, rows):
+    for r in range(PACK):
+        nc.sync.dma_start(out=plane[r:P:32, :].bitcast(I32), in_=rows[r : QUADRANTS * PACK : PACK, :].bitcast(I32))
 
 
 def deal_words(nc, dealt, raw):
@@ -54,8 +54,8 @@ def deal_scales(nc, dealt, raw):
 
 def deal_fours(nc, dealt, raw, tiles=slice(0, PACK)):
     nc.vector.tensor_copy(
-        out=dealt[:].bitcast(I32).rearrange("p (t a q w) -> p a t q w", t=tiles.stop - tiles.start, a=8, q=4),
-        in_=raw[:].bitcast(I32).rearrange("p (a q t w) -> p a t q w", t=PACK, a=8, q=4)[:, :, tiles],
+        out=dealt[:].bitcast(I32).rearrange("p (t a b w) -> p a t b w", t=tiles.stop - tiles.start, a=8, b=4),
+        in_=raw[:].bitcast(I32).rearrange("p (a b t w) -> p a t b w", t=PACK, a=8, b=4)[:, :, tiles],
     )
 
 
@@ -82,7 +82,9 @@ def tile_picked_aftlocal_none_po_kernel(
         w1s_raw = keep.tile([P, H], U8, name="w1s_raw", align_bytes=64)
         w3s_raw = keep.tile([P, N], U8, name="w3s_raw", align_bytes=64)
         w2_lo = keep.tile([P, 2, H], F32, name="w2_lo", align_bytes=64)
-        w2_hi = [keep.tile([P, 2, H // 2], F32, name="w2_hi%d" % b, tag="w2_hi%d" % b, align_bytes=64) for b in range(2)]
+        w2_hi = [
+            keep.tile([P, 2, H // 2], F32, name="w2_hi%d" % b, tag="w2_hi%d" % b, align_bytes=64) for b in range(2)
+        ]
         ident = keep.tile([P, P], F32, name="ident", align_bytes=64)
 
         nc.gpsimd.memset(xs[:, : T // 2].bitcast(I32), 0)
@@ -94,17 +96,17 @@ def tile_picked_aftlocal_none_po_kernel(
         nc.sync.dma_start(out=w1w_raw[:].bitcast(I32), in_=w1_words[0].bitcast(I32))
         nc.sync.dma_start(out=w3w_raw[:].bitcast(I32), in_=w3_words[0].bitcast(I32))
         x_rows = x_words[0].rearrange("p n t -> p (n t)").bitcast(I32)
-        load_scale_rows((nc.sync,), xs, x_scales[0])
+        load_scale_rows(nc, xs, x_scales[0])
         nc.sync.dma_start(out=xw[:].bitcast(I32), in_=x_rows)
         nc.sync.dma_start(lists[0][:], p1)
-        load_scale_rows((nc.sync,), w1s_raw, w1_scales[0])
+        load_scale_rows(nc, w1s_raw, w1_scales[0])
         w2_rows = w2.rearrange("(p j) c -> p j c", j=PACK)
         nc.sync.dma_start(out=w2_lo[:], in_=w2_rows[:, 0:2, :])
         for b in range(2):
             nc.sync.dma_start(out=w2_hi[b][:], in_=w2_rows[:, 2:4, tile_cols(b, H // 2)])
         nc.sync.dma_start(lists[1][:], p2)
         nc.sync.dma_start(lists[2][:], p3)
-        load_scale_rows((nc.sync,), w3s_raw, w3_scales[0])
+        load_scale_rows(nc, w3s_raw, w3_scales[0])
         make_identity(nc, ident[:])
 
         xg_s = keep.tile([P, S], U8, name="xg_s", align_bytes=64)
@@ -136,17 +138,10 @@ def tile_picked_aftlocal_none_po_kernel(
         w2q = keep.tile([P, H], U32, name="w2q", align_bytes=64)
         w2s = keep.tile([P, H], U8, name="w2s", align_bytes=64)
 
-        def round_w2(raw, rows, places, tiles=slice(0, PACK)):
+        def round_w2(raw, rows, columns, tiles=slice(0, PACK)):
             nc.vector.tensor_copy(
-                out=w2_bf[:, tiles, places, rows].rearrange("p t (q c) j -> p t q c j", c=PACK),
+                out=w2_bf[:, tiles, columns, rows].rearrange("p t (q c) j -> p t q c j", c=PACK),
                 in_=raw[:].rearrange("p j (q t c) -> p t q c j", t=PACK, c=PACK)[:, tiles],
-            )
-
-        def quantize_w2(t):
-            nc.vector.quantize_mx(
-                out=w2q[:, tile_cols(t)].bitcast(FP8X4),
-                scales=w2s[:, tile_cols(t)],
-                in_=w2_bf[:, t, :, :].rearrange("p m j -> p (m j)"),
             )
 
         round_w2(w2_lo, slice(0, 2), slice(0, P))
@@ -154,7 +149,11 @@ def tile_picked_aftlocal_none_po_kernel(
         round_w2(w2_hi[1], slice(2, 4), tile_cols(1, P // 2), slice(0, 2))
         round_w2(w2_hi[1], slice(2, 4), tile_cols(1, P // 2), slice(2, PACK))
         for t in range(PACK):
-            quantize_w2(t)
+            nc.vector.quantize_mx(
+                out=w2q[:, tile_cols(t)].bitcast(FP8X4),
+                scales=w2s[:, tile_cols(t)],
+                in_=w2_bf[:, t, :, :].rearrange("p m j -> p (m j)"),
+            )
         w1s.append(keep.tile([P, H // 2], U8, name="w1s1", tag="w2_bf", align_bytes=64))
         deal_fours(nc, w1s[1], w1s_raw, slice(2, PACK))
 
@@ -204,48 +203,44 @@ def tile_picked_aftlocal_none_po_kernel(
         y_scales = keep.tile([P, V], U8, name="y_scales", align_bytes=64)
         out_rows = out_0.rearrange("(p t) v -> p t v", t=PACK)
         out_words = out_1[0].rearrange("p v r -> p (v r)").bitcast(I32)
-        factor = []
+
+        def pair_of_sums(acc, u):
+            return acc[:].rearrange("v (t q u d) -> v u q t d", t=PACK, u=PAIRS, d=2)[:, u]
+
+        def like_sums(row):
+            return row.rearrange("v (q t d) -> v q t d", t=PACK, d=2)
+
+        roots, step = [], []
         for h in range(HALVES):
-            root = keep.tile([P, H], F32, name="root%d" % h, align_bytes=64)
-            other = keep.tile([P, H], F32, name="other%d" % h, align_bytes=64)
-            factor.append((root, other))
-            for u in range(2):
+            roots.append(keep.tile([P, H], F32, name="root%d" % h, align_bytes=64))
+            step.append(keep.tile([P, H], F32, name="other%d" % h, align_bytes=64))
+            for u in range(PAIRS):
                 pair = tile_cols(u, 2 * P)
-                nc.scalar.activation(
-                    root[:, pair].rearrange("v (q t d) -> v q t d", t=PACK, d=2),
-                    den[h][:].rearrange("v (t q u d) -> v u q t d", t=PACK, u=2, d=2)[:, u],
-                    ACT.Abs_reciprocal_sqrt,
-                )
+                nc.scalar.activation(like_sums(roots[h][:, pair]), pair_of_sums(den[h], u), ACT.Abs_reciprocal_sqrt)
                 if h == 0:
                     nc.vector.tensor_tensor(
-                        other[:, pair].rearrange("v (q t d) -> v q t d", t=PACK, d=2),
-                        num[h][:].rearrange("v (t q u d) -> v u q t d", t=PACK, u=2, d=2)[:, u],
-                        root[:, pair].rearrange("v (q t d) -> v q t d", t=PACK, d=2),
-                        MULT,
+                        like_sums(step[h][:, pair]), pair_of_sums(num[h], u), like_sums(roots[h][:, pair]), MULT
                     )
                 else:
-                    nc.scalar.activation(other[:, pair], root[:, pair], ACT.Square)
+                    nc.scalar.activation(step[h][:, pair], roots[h][:, pair], ACT.Square)
+
         for h in range(HALVES):
             places = tile_cols(h)
             z_turned = keep.tile([P, H], BF16, name="z_turned%d" % h, align_bytes=64)
             z_pairs = in_bank(TURN_BANKS[h], "z_pairs")
-            for u in range(2):
+            for u in range(PAIRS):
                 pair = tile_cols(u, 2 * P)
-                root, other = factor[h]
                 if h == 0:
-                    nc.vector.tensor_tensor(z_turned[:, pair], other[:, pair], root[:, pair], MULT)
+                    nc.vector.tensor_tensor(z_turned[:, pair], step[h][:, pair], roots[h][:, pair], MULT)
                 else:
                     nc.vector.tensor_tensor(
-                        z_turned[:, pair].rearrange("v (q t d) -> v q t d", t=PACK, d=2),
-                        num[h][:].rearrange("v (t q u d) -> v u q t d", t=PACK, u=2, d=2)[:, u],
-                        other[:, pair].rearrange("v (q t d) -> v q t d", t=PACK, d=2),
-                        MULT,
+                        like_sums(z_turned[:, pair]), pair_of_sums(num[h], u), like_sums(step[h][:, pair]), MULT
                     )
                 nc.tensor.transpose(z_pairs[:, tile_cols(u)], z_turned[:, pair].bitcast(F32), ident[:])
             z_bf = keep.tile([P, P * PACK], BF16, name="z_bf%d" % h, align_bytes=64)
             nc.scalar.copy(
-                out=z_bf[:].bitcast(F32).rearrange("p (v u) -> p v u", u=2),
-                in_=z_pairs[:, 0 : 2 * P].rearrange("p (u v) -> p v u", u=2),
+                out=z_bf[:].bitcast(F32).rearrange("p (v u) -> p v u", u=PAIRS),
+                in_=z_pairs[:, 0 : 2 * P].rearrange("p (u v) -> p v u", u=PAIRS),
             )
             zq = keep.tile([P, P], U32, name="zq%d" % h, align_bytes=64)
             zs = keep.tile([P, P], U8, name="zs%d" % h, align_bytes=64)
@@ -253,32 +248,23 @@ def tile_picked_aftlocal_none_po_kernel(
 
             y = keep.tile([P, PACK, P], F32, name="y%d" % h, align_bytes=64)
             y_bf = keep.tile([P, P, PACK], BF16, name="y_bf%d" % h, align_bytes=64)
-
-            def last_layer(acc, t):
-                nc.tensor.matmul_mx(
-                    out=acc,
-                    lhsT=w3w[:, tile_cols(t, 2 * P)].bitcast(FP4X4),
-                    lhsT_scale=w3s[:, tile_cols(t)],
-                    rhs=zq[:].bitcast(FP8X4),
-                    rhs_scale=zs[:],
-                    start=True,
-                    stop=True,
-                )
-
-            if h == HALVES - 1:
-                twin = in_bank(TWIN_BANK, "y_twin")
-                for t in range(PACK):
-                    last_layer(twin[:, tile_cols(t)], t)
-                nc.vector.tensor_copy(out=y_bf[:], in_=twin[:].rearrange("p (t v) -> p v t", t=PACK))
-            for u in range(2):
-                y_acc = in_bank(Y_BANKS[h][u], "y_acc")
-                for d in range(2):
-                    last_layer(y_acc[:, tile_cols(d)], 2 * u + d)
-                nc.scalar.copy(out=y[:, 2 * u : 2 * u + 2, :].rearrange("p t v -> p (t v)"), in_=y_acc[:, 0 : 2 * P])
+            for b, bank in enumerate(Y_BANKS[h]):
+                y_acc = in_bank(bank, "y_acc")
+                for i in range(2):
+                    t = 2 * b + i
+                    nc.tensor.matmul_mx(
+                        out=y_acc[:, tile_cols(i)],
+                        lhsT=w3w[:, tile_cols(t, 2 * P)].bitcast(FP4X4),
+                        lhsT_scale=w3s[:, tile_cols(t)],
+                        rhs=zq[:].bitcast(FP8X4),
+                        rhs_scale=zs[:],
+                        start=True,
+                        stop=True,
+                    )
+                nc.scalar.copy(out=y[:, 2 * b : 2 * b + 2, :].rearrange("p t v -> p (t v)"), in_=y_acc[:, 0 : 2 * P])
             nc.sync.dma_start(out=out_rows[:, :, places], in_=y[:])
 
-            if h < HALVES - 1:
-                nc.vector.tensor_copy(out=y_bf[:], in_=y[:].rearrange("p t v -> p v t"))
+            nc.vector.tensor_copy(out=y_bf[:], in_=y[:].rearrange("p t v -> p v t"))
             nc.vector.quantize_mx(
                 out=y_words[:, places].bitcast(FP8X4),
                 scales=y_scales[:, places],

@@ -164,6 +164,9 @@ def tile_picked_aftlocal_none_po_kernel(
             w2_codes = w2q[:, tile_cols(t)].bitcast(FP8X4)
             val_banks.append(project(in_bank(VAL_BANKS[t], "val_acc"), w2_codes, w2s[:, tile_cols(t)]))
         nc.scalar.copy(out=s_sb[0][:], in_=s_banks[0][:])
+        nc.scalar.copy(out=s_sb[1][:], in_=s_banks[1][:])
+        val_sb = [keep.tile([P, S], F32, name="val%d" % t, align_bytes=64) for t in range(PACK)]
+        nc.vector.tensor_copy(out=val_sb[0][:], in_=val_banks[0][:])
 
         def add_turned(acc, terms):
             for k in range(LISTS):
@@ -177,15 +180,19 @@ def tile_picked_aftlocal_none_po_kernel(
             ev = [keep.tile([P, V], F32, name="ev%d_%d" % (t, k), align_bytes=64) for k in range(LISTS)]
             for k in range(LISTS):
                 nc.scalar.activation(e[k][:], s_sb[t][:].indirect(lists[k][:]), ACT.Exp)
-            if not last:
-                nc.scalar.copy(out=s_sb[t + 1][:], in_=s_banks[t + 1][:])
-            val_t = keep.tile([P, S], F32, name="val%d" % t, align_bytes=64)
-            nc.vector.tensor_copy(out=val_t[:], in_=val_banks[t][:])
-            for h in range(HALVES):
-                add_turned(den[h][:, tile_cols(t)], [e[k][:, tile_cols(h)] for k in range(LISTS)])
+                if k == 0 and t in (1, 2):
+                    nc.scalar.copy(out=s_sb[t + 1][:], in_=s_banks[t + 1][:])
+            val_t = val_sb[t]
+            if last:
+                for h in range(HALVES):
+                    add_turned(den[h][:, tile_cols(t)], [e[k][:, tile_cols(h)] for k in range(LISTS)])
             if not last:
                 for k in range(LISTS):
                     nc.vector.tensor_tensor(ev[k][:], val_t[:].indirect(lists[k][:]), e[k][:], MULT)
+                    if k == 1:
+                        nc.vector.tensor_copy(out=val_sb[t + 1][:], in_=val_banks[t + 1][:])
+                for h in range(HALVES):
+                    add_turned(den[h][:, tile_cols(t)], [e[k][:, tile_cols(h)] for k in range(LISTS)])
                 for h in range(HALVES):
                     add_turned(num[h][:, tile_cols(t)], [ev[k][:, tile_cols(h)] for k in range(LISTS)])
             else:
@@ -199,6 +206,7 @@ def tile_picked_aftlocal_none_po_kernel(
         w3s = keep.tile([P, N], U8, name="w3s", tag="w2_hi1", align_bytes=64)
         deal_scales(nc, w3s, w3s_raw)
 
+        y = keep.tile([P, PACK, V], F32, name="y", align_bytes=64)
         y_words = keep.tile([P, V], U32, name="y_words", align_bytes=64)
         y_scales = keep.tile([P, V], U8, name="y_scales", align_bytes=64)
         out_rows = out_0.rearrange("(p t) v -> p t v", t=PACK)
@@ -246,8 +254,6 @@ def tile_picked_aftlocal_none_po_kernel(
             zs = keep.tile([P, P], U8, name="zs%d" % h, align_bytes=64)
             nc.vector.quantize_mx(out=zq[:].bitcast(FP8X4), scales=zs[:], in_=z_bf[:])
 
-            y = keep.tile([P, PACK, P], F32, name="y%d" % h, align_bytes=64)
-            y_bf = keep.tile([P, P, PACK], BF16, name="y_bf%d" % h, align_bytes=64)
             for b, bank in enumerate(Y_BANKS[h]):
                 y_acc = in_bank(bank, "y_acc")
                 for i in range(2):
@@ -261,14 +267,19 @@ def tile_picked_aftlocal_none_po_kernel(
                         start=True,
                         stop=True,
                     )
-                nc.scalar.copy(out=y[:, 2 * b : 2 * b + 2, :].rearrange("p t v -> p (t v)"), in_=y_acc[:, 0 : 2 * P])
-            nc.sync.dma_start(out=out_rows[:, :, places], in_=y[:])
+                nc.scalar.copy(out=y[:, 2 * b : 2 * b + 2, places], in_=y_acc[:, 0 : 2 * P].rearrange("p (t v) -> p t v", t=2))
+        for b in range(2):
+            nc.sync.dma_start(out=out_rows[:, 2 * b : 2 * b + 2, :], in_=y[:, 2 * b : 2 * b + 2, :])
 
-            nc.vector.tensor_copy(out=y_bf[:], in_=y[:].rearrange("p t v -> p v t"))
+        y_bf = [keep.tile([P, P, PACK], BF16, name="y_bf%d" % h, align_bytes=64) for h in range(HALVES)]
+        for h in range(HALVES):
+            nc.vector.tensor_copy(out=y_bf[h][:], in_=y[:, :, tile_cols(h)].rearrange("p t v -> p v t"))
+        for h in range(HALVES):
+            places = tile_cols(h)
             nc.vector.quantize_mx(
                 out=y_words[:, places].bitcast(FP8X4),
                 scales=y_scales[:, places],
-                in_=y_bf[:].rearrange("p v t -> p (v t)"),
+                in_=y_bf[h][:].rearrange("p v t -> p (v t)"),
             )
             nc.sync.dma_start(out=out_words[:, places], in_=y_words[:, places].bitcast(I32))
 

@@ -33,9 +33,11 @@ TURN_BANKS = (2, 3)
 Y_BANKS = ((6, 7), (4, 5))
 
 
-def load_scale_rows(nc, plane, rows):
+def load_scale_rows(queues, plane, rows):
     for r in range(PACK):
-        nc.sync.dma_start(out=plane[r:P:32, :].bitcast(I32), in_=rows[r : QUADRANTS * PACK : PACK, :].bitcast(I32))
+        queues[r % len(queues)].dma_start(
+            out=plane[r:P:32, :].bitcast(I32), in_=rows[r : QUADRANTS * PACK : PACK, :].bitcast(I32)
+        )
 
 
 def deal_words(nc, dealt, raw):
@@ -87,8 +89,8 @@ def tile_picked_aftlocal_none_po_kernel(
         ]
         ident = keep.tile([P, P], F32, name="ident", align_bytes=64)
 
-        nc.gpsimd.memset(xs[:, : T // 2].bitcast(I32), 0)
-        nc.vector.memset(xs[:, T // 2 :].bitcast(I32), 0)
+        nc.gpsimd.memset(xs[:, : 3 * T // 4].bitcast(I32), 0)
+        nc.vector.memset(xs[:, 3 * T // 4 :].bitcast(I32), 0)
         nc.vector.memset(w1s_raw[:].bitcast(I32), 0)
         nc.vector.memset(w3s_raw[:].bitcast(I32), 0)
 
@@ -96,17 +98,17 @@ def tile_picked_aftlocal_none_po_kernel(
         nc.sync.dma_start(out=w1w_raw[:].bitcast(I32), in_=w1_words[0].bitcast(I32))
         nc.sync.dma_start(out=w3w_raw[:].bitcast(I32), in_=w3_words[0].bitcast(I32))
         x_rows = x_words[0].rearrange("p n t -> p (n t)").bitcast(I32)
-        load_scale_rows(nc, xs, x_scales[0])
+        load_scale_rows((nc.scalar, nc.sync), xs, x_scales[0])
         nc.sync.dma_start(out=xw[:].bitcast(I32), in_=x_rows)
         nc.sync.dma_start(lists[0][:], p1)
-        load_scale_rows(nc, w1s_raw, w1_scales[0])
+        load_scale_rows((nc.sync,), w1s_raw, w1_scales[0])
         w2_rows = w2.rearrange("(p j) c -> p j c", j=PACK)
         nc.sync.dma_start(out=w2_lo[:], in_=w2_rows[:, 0:2, :])
         for b in range(2):
             nc.sync.dma_start(out=w2_hi[b][:], in_=w2_rows[:, 2:4, tile_cols(b, H // 2)])
         nc.sync.dma_start(lists[1][:], p2)
         nc.sync.dma_start(lists[2][:], p3)
-        load_scale_rows(nc, w3s_raw, w3_scales[0])
+        load_scale_rows((nc.sync,), w3s_raw, w3_scales[0])
         make_identity(nc, ident[:])
 
         xg_s = keep.tile([P, S], U8, name="xg_s", align_bytes=64)
@@ -273,7 +275,11 @@ def tile_picked_aftlocal_none_po_kernel(
 
         y_bf = [keep.tile([P, P, PACK], BF16, name="y_bf%d" % h, align_bytes=64) for h in range(HALVES)]
         for h in range(HALVES):
-            nc.vector.tensor_copy(out=y_bf[h][:], in_=y[:, :, tile_cols(h)].rearrange("p t v -> p v t"))
+            for b in range(2):
+                nc.vector.tensor_copy(
+                    out=y_bf[h][:, :, 2 * b : 2 * b + 2],
+                    in_=y[:, 2 * b : 2 * b + 2, tile_cols(h)].rearrange("p t v -> p v t"),
+                )
         for h in range(HALVES):
             places = tile_cols(h)
             nc.vector.quantize_mx(

@@ -23,6 +23,7 @@ LISTS = 3
 QUADRANTS = 4
 STRIPE = 16
 HALVES = V // P
+W2_PIECES = (slice(0, H // 2), slice(H // 2, 3 * H // 4), slice(3 * H // 4, H))
 PAIRS = 2
 
 S_BANKS = (0, 1, 2, 3)
@@ -83,9 +84,9 @@ def tile_picked_aftlocal_none_po_kernel(
         w3w_raw = keep.tile([P, 2 * N], U8, name="w3w_raw", align_bytes=64)
         w1s_raw = keep.tile([P, H], U8, name="w1s_raw", align_bytes=64)
         w3s_raw = keep.tile([P, N], U8, name="w3s_raw", align_bytes=64)
-        w2_lo = keep.tile([P, 2, H], F32, name="w2_lo", align_bytes=64)
-        w2_hi = [
-            keep.tile([P, 2, H // 2], F32, name="w2_hi%d" % b, tag="w2_hi%d" % b, align_bytes=64) for b in range(2)
+        w2_raw = [
+            keep.tile([P, PACK, piece.stop - piece.start], F32, name="w2_raw%d" % b, tag="w2_raw%d" % b, align_bytes=64)
+            for b, piece in enumerate(W2_PIECES)
         ]
         ident = keep.tile([P, P], F32, name="ident", align_bytes=64)
 
@@ -103,9 +104,8 @@ def tile_picked_aftlocal_none_po_kernel(
         nc.sync.dma_start(lists[0][:], p1)
         load_scale_rows((nc.sync,), w1s_raw, w1_scales[0])
         w2_rows = w2.rearrange("(p j) c -> p j c", j=PACK)
-        nc.sync.dma_start(out=w2_lo[:], in_=w2_rows[:, 0:2, :])
-        for b in range(2):
-            nc.sync.dma_start(out=w2_hi[b][:], in_=w2_rows[:, 2:4, tile_cols(b, H // 2)])
+        for raw, piece in zip(w2_raw, W2_PIECES):
+            nc.sync.dma_start(out=raw[:], in_=w2_rows[:, :, piece])
         nc.sync.dma_start(lists[1][:], p2)
         nc.sync.dma_start(lists[2][:], p3)
         load_scale_rows((nc.sync,), w3s_raw, w3_scales[0])
@@ -115,13 +115,13 @@ def tile_picked_aftlocal_none_po_kernel(
         xg_w = keep.tile([P, S], U32, name="xg_w", align_bytes=64)
         w1w = keep.tile([P, 2 * H], U8, name="w1w", align_bytes=64)
         w2_bf = keep.tile([P, PACK, P, PACK], BF16, name="w2_bf", tag="w2_bf", align_bytes=64)
-        w1s = [keep.tile([P, H // 2], U8, name="w1s0", align_bytes=64)]
+        w1s_early = keep.tile([P, (PACK - 1) * P], U8, name="w1s_early", align_bytes=64)
         w3w = keep.tile([P, 2 * N], U8, name="w3w", align_bytes=64)
         nc.vector.tensor_copy(xg_s[:], xs[:].indirect(offs_t[:]))
         deal_fours(nc, w1w, w1w_raw)
         deal_words(nc, w3w, w3w_raw)
         nc.vector.tensor_copy(xg_w[:], xw[:].indirect(offs_t[:]))
-        deal_fours(nc, w1s[0], w1s_raw, slice(0, 2))
+        deal_fours(nc, w1s_early, w1s_raw, slice(0, PACK - 1))
 
         def project(bank, codes, scales):
             nc.tensor.matmul_mx(
@@ -140,29 +140,31 @@ def tile_picked_aftlocal_none_po_kernel(
         w2q = keep.tile([P, H], U32, name="w2q", align_bytes=64)
         w2s = keep.tile([P, H], U8, name="w2s", align_bytes=64)
 
-        def round_w2(raw, rows, columns, tiles=slice(0, PACK)):
+        def round_w2(b, tiles):
+            columns = slice(W2_PIECES[b].start // PACK, W2_PIECES[b].stop // PACK)
             nc.vector.tensor_copy(
-                out=w2_bf[:, tiles, columns, rows].rearrange("p t (q c) j -> p t q c j", c=PACK),
-                in_=raw[:].rearrange("p j (q t c) -> p t q c j", t=PACK, c=PACK)[:, tiles],
+                out=w2_bf[:, tiles, columns, :].rearrange("p t (q c) j -> p t q j c", c=PACK),
+                in_=w2_raw[b][:].rearrange("p j (q t c) -> p t q j c", t=PACK, c=PACK)[:, tiles],
             )
 
-        round_w2(w2_lo, slice(0, 2), slice(0, P))
-        round_w2(w2_hi[0], slice(2, 4), tile_cols(0, P // 2))
-        round_w2(w2_hi[1], slice(2, 4), tile_cols(1, P // 2), slice(0, 2))
-        round_w2(w2_hi[1], slice(2, 4), tile_cols(1, P // 2), slice(2, PACK))
+        round_w2(0, slice(0, PACK))
+        round_w2(1, slice(0, PACK))
+        round_w2(2, slice(0, 2))
+        round_w2(2, slice(2, PACK))
         for t in range(PACK):
             nc.vector.quantize_mx(
                 out=w2q[:, tile_cols(t)].bitcast(FP8X4),
                 scales=w2s[:, tile_cols(t)],
                 in_=w2_bf[:, t, :, :].rearrange("p m j -> p (m j)"),
             )
-        w1s.append(keep.tile([P, H // 2], U8, name="w1s1", tag="w2_bf", align_bytes=64))
-        deal_fours(nc, w1s[1], w1s_raw, slice(2, PACK))
+        w1s_late = keep.tile([P, P], U8, name="w1s_late", tag="w2_bf", align_bytes=64)
+        deal_fours(nc, w1s_late, w1s_raw, slice(PACK - 1, PACK))
+        w1s = [w1s_early[:, tile_cols(t)] for t in range(PACK - 1)] + [w1s_late[:]]
 
         s_banks, val_banks = [], []
         for t in range(PACK):
             w1_codes = w1w[:, tile_cols(t, 2 * P)].bitcast(FP4X4)
-            s_banks.append(project(in_bank(S_BANKS[t], "s_acc"), w1_codes, w1s[t // 2][:, tile_cols(t % 2)]))
+            s_banks.append(project(in_bank(S_BANKS[t], "s_acc"), w1_codes, w1s[t]))
             w2_codes = w2q[:, tile_cols(t)].bitcast(FP8X4)
             val_banks.append(project(in_bank(VAL_BANKS[t], "val_acc"), w2_codes, w2s[:, tile_cols(t)]))
         nc.scalar.copy(out=s_sb[0][:], in_=s_banks[0][:])
@@ -205,7 +207,7 @@ def tile_picked_aftlocal_none_po_kernel(
                         nc.vector.tensor_tensor(ev[k][:, places], val_t[:].indirect(offsets), e[k][:, places], MULT)
                     add_turned(num[h][:, tile_cols(t)], [ev[k][:, places] for k in range(LISTS)])
 
-        w3s = keep.tile([P, N], U8, name="w3s", tag="w2_hi1", align_bytes=64)
+        w3s = keep.tile([P, N], U8, name="w3s", tag="w2_raw2", align_bytes=64)
         deal_scales(nc, w3s, w3s_raw)
 
         y = keep.tile([P, PACK, V], F32, name="y", align_bytes=64)

@@ -147,30 +147,38 @@ def tile_picked_aftlocal_none_po_kernel(
                 in_=w2_raw[b][:].rearrange("p j (q t c) -> p t q j c", t=PACK, c=PACK)[:, tiles],
             )
 
-        round_w2(0, slice(0, PACK))
-        round_w2(1, slice(0, PACK))
-        round_w2(2, slice(0, 2))
-        round_w2(2, slice(2, PACK))
-        for t in range(PACK):
+        def quantize_w2(t):
             nc.vector.quantize_mx(
                 out=w2q[:, tile_cols(t)].bitcast(FP8X4),
                 scales=w2s[:, tile_cols(t)],
                 in_=w2_bf[:, t, :, :].rearrange("p m j -> p (m j)"),
             )
-        w1s_late = keep.tile([P, P], U8, name="w1s_late", tag="w2_bf", align_bytes=64)
-        deal_fours(nc, w1s_late, w1s_raw, slice(PACK - 1, PACK))
-        w1s = [w1s_early[:, tile_cols(t)] for t in range(PACK - 1)] + [w1s_late[:]]
 
-        s_banks, val_banks = [], []
-        for t in range(PACK):
+        round_w2(0, slice(0, PACK))
+        round_w2(1, slice(0, PACK))
+        round_w2(2, slice(0, 1))
+        round_w2(2, slice(1, 2))
+        quantize_w2(0)
+        round_w2(2, slice(2, PACK))
+        for t in range(1, PACK):
+            quantize_w2(t)
+
+        def project_s(t, scales):
             w1_codes = w1w[:, tile_cols(t, 2 * P)].bitcast(FP4X4)
-            s_banks.append(project(in_bank(S_BANKS[t], "s_acc"), w1_codes, w1s[t]))
-            w2_codes = w2q[:, tile_cols(t)].bitcast(FP8X4)
-            val_banks.append(project(in_bank(VAL_BANKS[t], "val_acc"), w2_codes, w2s[:, tile_cols(t)]))
+            return project(in_bank(S_BANKS[t], "s_acc"), w1_codes, scales)
+
+        s_banks = [project_s(t, w1s_early[:, tile_cols(t)]) for t in range(PACK - 1)]
+        val_banks = [
+            project(in_bank(VAL_BANKS[t], "val_acc"), w2q[:, tile_cols(t)].bitcast(FP8X4), w2s[:, tile_cols(t)])
+            for t in range(PACK)
+        ]
         nc.scalar.copy(out=s_sb[0][:], in_=s_banks[0][:])
         nc.scalar.copy(out=s_sb[1][:], in_=s_banks[1][:])
         val_sb = [keep.tile([P, S], F32, name="val%d" % t, align_bytes=64) for t in range(PACK)]
         nc.vector.tensor_copy(out=val_sb[0][:], in_=val_banks[0][:])
+        w1s_late = keep.tile([P, P], U8, name="w1s_late", tag="w2_bf", align_bytes=64)
+        deal_fours(nc, w1s_late, w1s_raw, slice(PACK - 1, PACK))
+        s_banks.append(project_s(PACK - 1, w1s_late[:]))
 
         def add_turned(acc, terms):
             for k in range(LISTS):
@@ -207,8 +215,6 @@ def tile_picked_aftlocal_none_po_kernel(
                         nc.vector.tensor_tensor(ev[k][:, places], val_t[:].indirect(offsets), e[k][:, places], MULT)
                     add_turned(num[h][:, tile_cols(t)], [ev[k][:, places] for k in range(LISTS)])
 
-        w3s = keep.tile([P, N], U8, name="w3s", tag="w2_raw2", align_bytes=64)
-        deal_scales(nc, w3s, w3s_raw)
 
         y = keep.tile([P, PACK, V], F32, name="y", align_bytes=64)
         y_words = keep.tile([P, V], U32, name="y_words", align_bytes=64)
@@ -236,10 +242,11 @@ def tile_picked_aftlocal_none_po_kernel(
                 else:
                     nc.scalar.activation(step[h][:, pair], roots[h][:, pair], ACT.Square)
 
+        turned = []
         for h in range(HALVES):
-            places = tile_cols(h)
             z_turned = keep.tile([P, H], BF16, name="z_turned%d" % h, align_bytes=64)
             z_pairs = in_bank(TURN_BANKS[h], "z_pairs")
+            turned.append(z_pairs)
             for u in range(PAIRS):
                 pair = tile_cols(u, 2 * P)
                 if h == 0:
@@ -249,6 +256,13 @@ def tile_picked_aftlocal_none_po_kernel(
                         like_sums(z_turned[:, pair]), pair_of_sums(num[h], u), like_sums(step[h][:, pair]), MULT
                     )
                 nc.tensor.transpose(z_pairs[:, tile_cols(u)], z_turned[:, pair].bitcast(F32), ident[:])
+
+        w3s = keep.tile([P, N], U8, name="w3s", tag="other1", align_bytes=64)
+        deal_scales(nc, w3s, w3s_raw)
+
+        for h in range(HALVES):
+            places = tile_cols(h)
+            z_pairs = turned[h]
             z_bf = keep.tile([P, P * PACK], BF16, name="z_bf%d" % h, align_bytes=64)
             nc.scalar.copy(
                 out=z_bf[:].bitcast(F32).rearrange("p (v u) -> p v u", u=PAIRS),

@@ -23,7 +23,7 @@ LISTS = 3
 QUADRANTS = 4
 STRIPE = 16
 HALVES = V // P
-W2_PIECES = (slice(0, H // 2), slice(H // 2, 3 * H // 4), slice(3 * H // 4, H))
+W2_PIECES = (slice(0, H // 2), slice(H // 2, 13 * H // 16), slice(13 * H // 16, H))
 PAIRS = 2
 
 S_BANKS = (0, 1, 2, 3)
@@ -194,6 +194,8 @@ def tile_picked_aftlocal_none_po_kernel(
                 nc.scalar.activation(e[k][:], s_sb[t][:].indirect(lists[k][:]), ACT.Exp)
                 if k == 0 and t in (1, 2):
                     nc.scalar.copy(out=s_sb[t + 1][:], in_=s_banks[t + 1][:])
+                if k == 1 and t == 1:
+                    nc.scalar.copy(out=val_sb[PACK - 1][:, : S // 4], in_=val_banks[PACK - 1][:, : S // 4])
             val_t = val_sb[t]
             if last:
                 for h in range(HALVES):
@@ -202,7 +204,8 @@ def tile_picked_aftlocal_none_po_kernel(
                 for k in range(LISTS):
                     nc.vector.tensor_tensor(ev[k][:], val_t[:].indirect(lists[k][:]), e[k][:], MULT)
                     if k == 1:
-                        nc.vector.tensor_copy(out=val_sb[t + 1][:], in_=val_banks[t + 1][:])
+                        rest = slice(S // 4 if t + 1 == PACK - 1 else 0, S)
+                        nc.vector.tensor_copy(out=val_sb[t + 1][:, rest], in_=val_banks[t + 1][:, rest])
                 for h in range(HALVES):
                     add_turned(den[h][:, tile_cols(t)], [e[k][:, tile_cols(h)] for k in range(LISTS)])
                 for h in range(HALVES):

@@ -219,7 +219,7 @@ def tile_picked_aftlocal_none_po_kernel(
                     add_turned(num[h][:, tile_cols(t)], [ev[k][:, places] for k in range(LISTS)])
 
 
-        y = keep.tile([P, PACK, V], F32, name="y", align_bytes=64)
+        y = [keep.tile([P, PACK, P], F32, name="y%d" % h, align_bytes=64) for h in range(HALVES)]
         y_words = keep.tile([P, V], U32, name="y_words", align_bytes=64)
         y_scales = keep.tile([P, V], U8, name="y_scales", align_bytes=64)
         out_rows = out_0.rearrange("(p t) v -> p t v", t=PACK)
@@ -263,6 +263,7 @@ def tile_picked_aftlocal_none_po_kernel(
         w3s = keep.tile([P, N], U8, name="w3s", tag="other1", align_bytes=64)
         deal_scales(nc, w3s, w3s_raw)
 
+        y_bf = [keep.tile([P, P, PACK], BF16, name="y_bf%d" % h, align_bytes=64) for h in range(HALVES)]
         for h in range(HALVES):
             places = tile_cols(h)
             z_pairs = turned[h]
@@ -288,17 +289,20 @@ def tile_picked_aftlocal_none_po_kernel(
                         start=True,
                         stop=True,
                     )
-                nc.scalar.copy(out=y[:, 2 * b : 2 * b + 2, places], in_=y_acc[:, 0 : 2 * P].rearrange("p (t v) -> p t v", t=2))
+                nc.scalar.copy(out=y[h][:, 2 * b : 2 * b + 2, :], in_=y_acc[:, 0 : 2 * P].rearrange("p (t v) -> p t v", t=2))
+                if (h, b) == (1, 1):
+                    nc.scalar.copy(
+                        out=y_bf[h][:, :, 2 * b : 2 * b + 2], in_=y_acc[:, 0 : 2 * P].rearrange("p (t v) -> p v t", t=2)
+                    )
+        nc.sync.dma_start(out=out_rows[:, :, 0:P], in_=y[0][:])
         for b in range(2):
-            nc.sync.dma_start(out=out_rows[:, 2 * b : 2 * b + 2, :], in_=y[:, 2 * b : 2 * b + 2, :])
+            nc.sync.dma_start(out=out_rows[:, 2 * b : 2 * b + 2, P:V], in_=y[1][:, 2 * b : 2 * b + 2, :])
 
-        y_bf = [keep.tile([P, P, PACK], BF16, name="y_bf%d" % h, align_bytes=64) for h in range(HALVES)]
-        for h in range(HALVES):
-            for b in range(2):
-                nc.vector.tensor_copy(
-                    out=y_bf[h][:, :, 2 * b : 2 * b + 2],
-                    in_=y[:, 2 * b : 2 * b + 2, tile_cols(h)].rearrange("p t v -> p v t"),
-                )
+        for h, b in ((0, 0), (0, 1), (1, 0)):
+            nc.vector.tensor_copy(
+                out=y_bf[h][:, :, 2 * b : 2 * b + 2],
+                in_=y[h][:, 2 * b : 2 * b + 2, :].rearrange("p t v -> p v t"),
+            )
         for h in range(HALVES):
             places = tile_cols(h)
             nc.vector.quantize_mx(
@@ -306,7 +310,7 @@ def tile_picked_aftlocal_none_po_kernel(
                 scales=y_scales[:, places],
                 in_=y_bf[h][:].rearrange("p v t -> p (v t)"),
             )
-            nc.sync.dma_start(out=out_words[:, places], in_=y_words[:, places].bitcast(I32))
+        nc.sync.dma_start(out=out_words, in_=y_words[:].bitcast(I32))
 
         for q in range(QUADRANTS):
             queue = (nc.sync, nc.scalar)[q % 2]

@@ -289,11 +289,11 @@ def tile_picked_aftlocal_none_po_kernel(
                         start=True,
                         stop=True,
                     )
-                nc.scalar.copy(out=y[h][:, 2 * b : 2 * b + 2, :], in_=y_acc[:, 0 : 2 * P].rearrange("p (t v) -> p t v", t=2))
                 if (h, b) == (1, 1):
                     nc.scalar.copy(
                         out=y_bf[h][:, :, 2 * b : 2 * b + 2], in_=y_acc[:, 0 : 2 * P].rearrange("p (t v) -> p v t", t=2)
                     )
+                nc.scalar.copy(out=y[h][:, 2 * b : 2 * b + 2, :], in_=y_acc[:, 0 : 2 * P].rearrange("p (t v) -> p t v", t=2))
         nc.sync.dma_start(out=out_rows[:, :, 0:P], in_=y[0][:])
         for b in range(2):
             nc.sync.dma_start(out=out_rows[:, 2 * b : 2 * b + 2, P:V], in_=y[1][:, 2 * b : 2 * b + 2, :])

@@ -123,13 +123,13 @@ def tile_picked_aftlocal_none_po_kernel(
         nc.vector.tensor_copy(xg_w[:], xw[:].indirect(offs_t[:]))
         deal_fours(nc, w1s_early, w1s_raw, slice(0, PACK - 1))
 
-        def project(bank, codes, scales):
+        def project(bank, codes, scales, tokens=slice(0, S)):
             nc.tensor.matmul_mx(
-                out=bank[:],
+                out=bank[:, tokens],
                 lhsT=codes,
                 lhsT_scale=scales,
-                rhs=xg_w[:].bitcast(FP8X4),
-                rhs_scale=xg_s[:],
+                rhs=xg_w[:, tokens].bitcast(FP8X4),
+                rhs_scale=xg_s[:, tokens],
                 start=True,
                 stop=True,
             )
@@ -168,14 +168,17 @@ def tile_picked_aftlocal_none_po_kernel(
             return project(in_bank(S_BANKS[t], "s_acc"), w1_codes, scales)
 
         s_banks = [project_s(t, w1s_early[:, tile_cols(t)]) for t in range(PACK - 1)]
-        val_banks = [
-            project(in_bank(VAL_BANKS[t], "val_acc"), w2q[:, tile_cols(t)].bitcast(FP8X4), w2s[:, tile_cols(t)])
-            for t in range(PACK)
-        ]
+        def project_val(t, bank, tokens):
+            return project(in_bank(bank, "val_acc"), w2q[:, tile_cols(t)].bitcast(FP8X4), w2s[:, tile_cols(t)], tokens)
+
+        first, second = slice(0, S // 2), slice(S // 2, S)
+        val_first = project_val(0, S_BANKS[PACK - 1], first)
+        val_banks = [project_val(t, VAL_BANKS[t], second if t == 0 else slice(0, S)) for t in range(PACK)]
         nc.scalar.copy(out=s_sb[0][:], in_=s_banks[0][:])
         nc.scalar.copy(out=s_sb[1][:], in_=s_banks[1][:])
         val_sb = [keep.tile([P, S], F32, name="val%d" % t, align_bytes=64) for t in range(PACK)]
-        nc.vector.tensor_copy(out=val_sb[0][:], in_=val_banks[0][:])
+        nc.vector.tensor_copy(out=val_sb[0][:, first], in_=val_first[:, first])
+        nc.vector.tensor_copy(out=val_sb[0][:, second], in_=val_banks[0][:, second])
         w1s_late = keep.tile([P, P], U8, name="w1s_late", tag="w2_bf", align_bytes=64)
         deal_fours(nc, w1s_late, w1s_raw, slice(PACK - 1, PACK))
         s_banks.append(project_s(PACK - 1, w1s_late[:]))
@@ -194,8 +197,6 @@ def tile_picked_aftlocal_none_po_kernel(
                 nc.scalar.activation(e[k][:], s_sb[t][:].indirect(lists[k][:]), ACT.Exp)
                 if k == 0 and t in (1, 2):
                     nc.scalar.copy(out=s_sb[t + 1][:], in_=s_banks[t + 1][:])
-                if k == 1 and t == 1:
-                    nc.scalar.copy(out=val_sb[PACK - 1][:, : S // 4], in_=val_banks[PACK - 1][:, : S // 4])
             val_t = val_sb[t]
             if last:
                 for h in range(HALVES):
@@ -204,8 +205,7 @@ def tile_picked_aftlocal_none_po_kernel(
                 for k in range(LISTS):
                     nc.vector.tensor_tensor(ev[k][:], val_t[:].indirect(lists[k][:]), e[k][:], MULT)
                     if k == 1:
-                        rest = slice(S // 4 if t + 1 == PACK - 1 else 0, S)
-                        nc.vector.tensor_copy(out=val_sb[t + 1][:, rest], in_=val_banks[t + 1][:, rest])
+                        nc.vector.tensor_copy(out=val_sb[t + 1][:], in_=val_banks[t + 1][:])
                 for h in range(HALVES):
                     add_turned(den[h][:, tile_cols(t)], [e[k][:, tile_cols(h)] for k in range(LISTS)])
                 for h in range(HALVES):
@@ -234,16 +234,16 @@ def tile_picked_aftlocal_none_po_kernel(
         roots, step = [], []
         for h in range(HALVES):
             roots.append(keep.tile([P, H], F32, name="root%d" % h, align_bytes=64))
-            step.append(keep.tile([P, H], F32, name="other%d" % h, align_bytes=64))
+            step.append([keep.tile([P, 2 * P], F32, name="other%d_%d" % (h, u), align_bytes=64) for u in range(PAIRS)])
             for u in range(PAIRS):
                 pair = tile_cols(u, 2 * P)
                 nc.scalar.activation(like_sums(roots[h][:, pair]), pair_of_sums(den[h], u), ACT.Abs_reciprocal_sqrt)
                 if h == 0:
                     nc.vector.tensor_tensor(
-                        like_sums(step[h][:, pair]), pair_of_sums(num[h], u), like_sums(roots[h][:, pair]), MULT
+                        like_sums(step[h][u][:]), pair_of_sums(num[h], u), like_sums(roots[h][:, pair]), MULT
                     )
                 else:
-                    nc.scalar.activation(step[h][:, pair], roots[h][:, pair], ACT.Square)
+                    nc.scalar.activation(step[h][u][:], roots[h][:, pair], ACT.Square)
 
         turned = []
         for h in range(HALVES):
@@ -253,14 +253,14 @@ def tile_picked_aftlocal_none_po_kernel(
             for u in range(PAIRS):
                 pair = tile_cols(u, 2 * P)
                 if h == 0:
-                    nc.vector.tensor_tensor(z_turned[:, pair], step[h][:, pair], roots[h][:, pair], MULT)
+                    nc.vector.tensor_tensor(z_turned[:, pair], step[h][u][:], roots[h][:, pair], MULT)
                 else:
                     nc.vector.tensor_tensor(
-                        like_sums(z_turned[:, pair]), pair_of_sums(num[h], u), like_sums(step[h][:, pair]), MULT
+                        like_sums(z_turned[:, pair]), pair_of_sums(num[h], u), like_sums(step[h][u][:]), MULT
                     )
                 nc.tensor.transpose(z_pairs[:, tile_cols(u)], z_turned[:, pair].bitcast(F32), ident[:])
 
-        w3s = keep.tile([P, N], U8, name="w3s", tag="other1", align_bytes=64)
+        w3s = keep.tile([P, N], U8, name="w3s", tag="other1_0", align_bytes=64)
         deal_scales(nc, w3s, w3s_raw)
 
         y_bf = [keep.tile([P, P, PACK], BF16, name="y_bf%d" % h, align_bytes=64) for h in range(HALVES)]
@@ -298,11 +298,10 @@ def tile_picked_aftlocal_none_po_kernel(
         for b in range(2):
             nc.sync.dma_start(out=out_rows[:, 2 * b : 2 * b + 2, P:V], in_=y[1][:, 2 * b : 2 * b + 2, :])
 
-        for h, b in ((0, 0), (0, 1), (1, 0)):
-            nc.vector.tensor_copy(
-                out=y_bf[h][:, :, 2 * b : 2 * b + 2],
-                in_=y[h][:, 2 * b : 2 * b + 2, :].rearrange("p t v -> p v t"),
-            )
+        nc.vector.tensor_copy(
+            out=y_bf[0][:].rearrange("p (c i) t -> p c t i", i=4), in_=y[0][:].rearrange("p t (c i) -> p c t i", i=4)
+        )
+        nc.vector.tensor_copy(out=y_bf[1][:, :, 0:2], in_=y[1][:, 0:2, :].rearrange("p t v -> p v t"))
         for h in range(HALVES):
             places = tile_cols(h)
             nc.vector.quantize_mx(

@@ -42,9 +42,9 @@ def load_scale_rows(queues, plane, rows):
 
 
 def deal_words(nc, dealt, raw):
-    nc.vector.tensor_copy(
-        out=dealt[:].rearrange("p (t a m b) -> p a t m b", t=PACK, m=8, b=2),
-        in_=raw[:].rearrange("p (a m t b) -> p a t m b", t=PACK, m=8, b=2),
+    nc.scalar.copy(
+        out=dealt[:].bitcast(U16).rearrange("p (t a m) -> p a t m", t=PACK, m=8),
+        in_=raw[:].bitcast(U16).rearrange("p (a m t) -> p a t m", t=PACK, m=8),
     )
 
 
@@ -90,24 +90,23 @@ def tile_picked_aftlocal_none_po_kernel(
         ]
         ident = keep.tile([P, P], F32, name="ident", align_bytes=64)
 
-        nc.gpsimd.memset(xs[:, : 3 * T // 4].bitcast(I32), 0)
-        nc.vector.memset(xs[:, 3 * T // 4 :].bitcast(I32), 0)
+        nc.vector.memset(xs[:].bitcast(I32), 0)
         nc.vector.memset(w1s_raw[:].bitcast(I32), 0)
         nc.vector.memset(w3s_raw[:].bitcast(I32), 0)
 
         nc.sync.dma_start(offs_t[:], offs)
         nc.sync.dma_start(out=w1w_raw[:].bitcast(I32), in_=w1_words[0].bitcast(I32))
-        nc.sync.dma_start(out=w3w_raw[:].bitcast(I32), in_=w3_words[0].bitcast(I32))
+        nc.sync.dma_start(lists[0][:], p1)
         x_rows = x_words[0].rearrange("p n t -> p (n t)").bitcast(I32)
         load_scale_rows((nc.scalar, nc.sync), xs, x_scales[0])
         nc.sync.dma_start(out=xw[:].bitcast(I32), in_=x_rows)
-        nc.sync.dma_start(lists[0][:], p1)
         load_scale_rows((nc.sync,), w1s_raw, w1_scales[0])
         w2_rows = w2.rearrange("(p j) c -> p j c", j=PACK)
         for raw, piece in zip(w2_raw, W2_PIECES):
             nc.sync.dma_start(out=raw[:], in_=w2_rows[:, :, piece])
         nc.sync.dma_start(lists[1][:], p2)
         nc.sync.dma_start(lists[2][:], p3)
+        nc.sync.dma_start(out=w3w_raw[:].bitcast(I32), in_=w3_words[0].bitcast(I32))
         load_scale_rows((nc.sync,), w3s_raw, w3_scales[0])
         make_identity(nc, ident[:])
 
@@ -116,10 +115,8 @@ def tile_picked_aftlocal_none_po_kernel(
         w1w = keep.tile([P, 2 * H], U8, name="w1w", align_bytes=64)
         w2_bf = keep.tile([P, PACK, P, PACK], BF16, name="w2_bf", tag="w2_bf", align_bytes=64)
         w1s_early = keep.tile([P, (PACK - 1) * P], U8, name="w1s_early", align_bytes=64)
-        w3w = keep.tile([P, 2 * N], U8, name="w3w", align_bytes=64)
         nc.vector.tensor_copy(xg_s[:], xs[:].indirect(offs_t[:]))
         deal_fours(nc, w1w, w1w_raw)
-        deal_words(nc, w3w, w3w_raw)
         nc.vector.tensor_copy(xg_w[:], xw[:].indirect(offs_t[:]))
         deal_fours(nc, w1s_early, w1s_raw, slice(0, PACK - 1))
 
@@ -197,6 +194,8 @@ def tile_picked_aftlocal_none_po_kernel(
                 nc.scalar.activation(e[k][:], s_sb[t][:].indirect(lists[k][:]), ACT.Exp)
                 if k == 0 and t in (1, 2):
                     nc.scalar.copy(out=s_sb[t + 1][:], in_=s_banks[t + 1][:])
+                if k == 1 and t == 1:
+                    nc.scalar.copy(out=val_sb[PACK - 1][:, : S // 4], in_=val_banks[PACK - 1][:, : S // 4])
             val_t = val_sb[t]
             if last:
                 for h in range(HALVES):
@@ -205,7 +204,8 @@ def tile_picked_aftlocal_none_po_kernel(
                 for k in range(LISTS):
                     nc.vector.tensor_tensor(ev[k][:], val_t[:].indirect(lists[k][:]), e[k][:], MULT)
                     if k == 1:
-                        nc.vector.tensor_copy(out=val_sb[t + 1][:], in_=val_banks[t + 1][:])
+                        rest = slice(S // 4 if t + 1 == PACK - 1 else 0, S)
+                        nc.vector.tensor_copy(out=val_sb[t + 1][:, rest], in_=val_banks[t + 1][:, rest])
                 for h in range(HALVES):
                     add_turned(den[h][:, tile_cols(t)], [e[k][:, tile_cols(h)] for k in range(LISTS)])
                 for h in range(HALVES):
@@ -260,6 +260,8 @@ def tile_picked_aftlocal_none_po_kernel(
                     )
                 nc.tensor.transpose(z_pairs[:, tile_cols(u)], z_turned[:, pair].bitcast(F32), ident[:])
 
+        w3w = keep.tile([P, 2 * N], U8, name="w3w", tag="root0", align_bytes=64)
+        deal_words(nc, w3w, w3w_raw)
         w3s = keep.tile([P, N], U8, name="w3s", tag="other1_0", align_bytes=64)
         deal_scales(nc, w3s, w3s_raw)
 

@@ -41,10 +41,10 @@ def load_scale_rows(queues, plane, rows):
         )
 
 
-def deal_words(nc, dealt, raw):
+def deal_words(nc, dealt, raw, tiles):
     nc.scalar.copy(
-        out=dealt[:].bitcast(U16).rearrange("p (t a m) -> p a t m", t=PACK, m=8),
-        in_=raw[:].bitcast(U16).rearrange("p (a m t) -> p a t m", t=PACK, m=8),
+        out=dealt[:].bitcast(U16).rearrange("p (t a m) -> p a t m", t=tiles.stop - tiles.start, m=8),
+        in_=raw[:].bitcast(U16).rearrange("p (a m t) -> p a t m", t=PACK, m=8)[:, :, tiles],
     )
 
 
@@ -247,7 +247,7 @@ def tile_picked_aftlocal_none_po_kernel(
 
         turned = []
         for h in range(HALVES):
-            z_turned = keep.tile([P, H], BF16, name="z_turned%d" % h, align_bytes=64)
+            z_turned = keep.tile([P, H], BF16, name="z_turned%d" % h, tag="z_turned%d" % h, align_bytes=64)
             z_pairs = in_bank(TURN_BANKS[h], "z_pairs")
             turned.append(z_pairs)
             for u in range(PAIRS):
@@ -260,8 +260,8 @@ def tile_picked_aftlocal_none_po_kernel(
                     )
                 nc.tensor.transpose(z_pairs[:, tile_cols(u)], z_turned[:, pair].bitcast(F32), ident[:])
 
-        w3w = keep.tile([P, 2 * N], U8, name="w3w", tag="root0", align_bytes=64)
-        deal_words(nc, w3w, w3w_raw)
+        w3w = [keep.tile([P, N], U8, name="w3w0", tag="root0", align_bytes=64)]
+        deal_words(nc, w3w[0], w3w_raw, slice(0, 2))
         w3s = keep.tile([P, N], U8, name="w3s", tag="other1_0", align_bytes=64)
         deal_scales(nc, w3s, w3s_raw)
 
@@ -274,6 +274,9 @@ def tile_picked_aftlocal_none_po_kernel(
                 out=z_bf[:].bitcast(F32).rearrange("p (v u) -> p v u", u=PAIRS),
                 in_=z_pairs[:, 0 : 2 * P].rearrange("p (u v) -> p v u", u=PAIRS),
             )
+            if h == 0:
+                w3w.append(keep.tile([P, N], U8, name="w3w1", tag="z_turned0", align_bytes=64))
+                deal_words(nc, w3w[1], w3w_raw, slice(2, PACK))
             zq = keep.tile([P, P], U32, name="zq%d" % h, align_bytes=64)
             zs = keep.tile([P, P], U8, name="zs%d" % h, align_bytes=64)
             nc.vector.quantize_mx(out=zq[:].bitcast(FP8X4), scales=zs[:], in_=z_bf[:])
@@ -284,7 +287,7 @@ def tile_picked_aftlocal_none_po_kernel(
                     t = 2 * b + i
                     nc.tensor.matmul_mx(
                         out=y_acc[:, tile_cols(i)],
-                        lhsT=w3w[:, tile_cols(t, 2 * P)].bitcast(FP4X4),
+                        lhsT=w3w[b][:, tile_cols(i, 2 * P)].bitcast(FP4X4),
                         lhsT_scale=w3s[:, tile_cols(t)],
                         rhs=zq[:].bitcast(FP8X4),
                         rhs_scale=zs[:],
@@ -295,7 +298,8 @@ def tile_picked_aftlocal_none_po_kernel(
                     nc.scalar.copy(
                         out=y_bf[h][:, :, 2 * b : 2 * b + 2], in_=y_acc[:, 0 : 2 * P].rearrange("p (t v) -> p v t", t=2)
                     )
-                nc.scalar.copy(out=y[h][:, 2 * b : 2 * b + 2, :], in_=y_acc[:, 0 : 2 * P].rearrange("p (t v) -> p t v", t=2))
+                copy = nc.vector.tensor_copy if (h, b) == (0, 0) else nc.scalar.copy
+                copy(out=y[h][:, 2 * b : 2 * b + 2, :], in_=y_acc[:, 0 : 2 * P].rearrange("p (t v) -> p t v", t=2))
         nc.sync.dma_start(out=out_rows[:, :, 0:P], in_=y[0][:])
         for b in range(2):
             nc.sync.dma_start(out=out_rows[:, 2 * b : 2 * b + 2, P:V], in_=y[1][:, 2 * b : 2 * b + 2, :])

@@ -113,7 +113,10 @@ def tile_picked_aftlocal_none_po_kernel(
         xg_s = keep.tile([P, S], U8, name="xg_s", align_bytes=64)
         xg_w = keep.tile([P, S], U32, name="xg_w", align_bytes=64)
         w1w = keep.tile([P, 2 * H], U8, name="w1w", align_bytes=64)
-        w2_bf = keep.tile([P, PACK, P, PACK], BF16, name="w2_bf", tag="w2_bf", align_bytes=64)
+        w2_bf = [
+            keep.tile([P, PACK, P // 2, PACK], BF16, name="w2_bf%d" % g, tag="w2_bf%d" % g, align_bytes=64)
+            for g in range(2)
+        ]
         w1s_early = keep.tile([P, (PACK - 1) * P], U8, name="w1s_early", align_bytes=64)
         nc.vector.tensor_copy(xg_s[:], xs[:].indirect(offs_t[:]))
         deal_fours(nc, w1w, w1w_raw)
@@ -138,47 +141,53 @@ def tile_picked_aftlocal_none_po_kernel(
         w2s = keep.tile([P, H], U8, name="w2s", align_bytes=64)
 
         def round_w2(b, tiles):
-            columns = slice(W2_PIECES[b].start // PACK, W2_PIECES[b].stop // PACK)
+            g, start = divmod(W2_PIECES[b].start, H // 2)
+            columns = slice(start // PACK, (W2_PIECES[b].stop - g * H // 2) // PACK)
             nc.vector.tensor_copy(
-                out=w2_bf[:, tiles, columns, :].rearrange("p t (q c) j -> p t q j c", c=PACK),
+                out=w2_bf[g][:, tiles, columns, :].rearrange("p t (q c) j -> p t q j c", c=PACK),
                 in_=w2_raw[b][:].rearrange("p j (q t c) -> p t q j c", t=PACK, c=PACK)[:, tiles],
             )
 
-        def quantize_w2(t):
+        def quantize_w2(g, t):
+            columns = slice(P * t + P // 2 * g, P * t + P // 2 * (g + 1))
             nc.vector.quantize_mx(
-                out=w2q[:, tile_cols(t)].bitcast(FP8X4),
-                scales=w2s[:, tile_cols(t)],
-                in_=w2_bf[:, t, :, :].rearrange("p m j -> p (m j)"),
+                out=w2q[:, columns].bitcast(FP8X4),
+                scales=w2s[:, columns],
+                in_=w2_bf[g][:, t].rearrange("p m j -> p (m j)"),
             )
 
         round_w2(0, slice(0, PACK))
         round_w2(1, slice(0, PACK))
+        for t in range(PACK):
+            quantize_w2(0, t)
         round_w2(2, slice(0, 1))
-        round_w2(2, slice(1, 2))
-        quantize_w2(0)
-        round_w2(2, slice(2, PACK))
-        for t in range(1, PACK):
-            quantize_w2(t)
+        round_w2(2, slice(1, PACK))
+        for t in range(PACK):
+            quantize_w2(1, t)
 
-        def project_s(t, scales):
+        def project_s(t, scales, bank, tokens=slice(0, S)):
             w1_codes = w1w[:, tile_cols(t, 2 * P)].bitcast(FP4X4)
-            return project(in_bank(S_BANKS[t], "s_acc"), w1_codes, scales)
+            return project(in_bank(bank, "s_acc"), w1_codes, scales, tokens)
 
-        s_banks = [project_s(t, w1s_early[:, tile_cols(t)]) for t in range(PACK - 1)]
+        first, second = slice(0, S // 2), slice(S // 2, S)
+        s_banks = [project_s(t, w1s_early[:, tile_cols(t)], S_BANKS[t]) for t in range(2)]
+        s_banks.append(project_s(2, w1s_early[:, tile_cols(2)], S_BANKS[2], first))
+        nc.scalar.copy(out=s_sb[0][:], in_=s_banks[0][:])
+        nc.scalar.copy(out=s_sb[1][:], in_=s_banks[1][:])
+        s2_second = project_s(2, w1s_early[:, tile_cols(2)], S_BANKS[0], second)
+        nc.vector.tensor_copy(out=s_sb[2][:, second], in_=s2_second[:, second])
+
         def project_val(t, bank, tokens):
             return project(in_bank(bank, "val_acc"), w2q[:, tile_cols(t)].bitcast(FP8X4), w2s[:, tile_cols(t)], tokens)
 
-        first, second = slice(0, S // 2), slice(S // 2, S)
         val_first = project_val(0, S_BANKS[PACK - 1], first)
         val_banks = [project_val(t, VAL_BANKS[t], second if t == 0 else slice(0, S)) for t in range(PACK)]
-        nc.scalar.copy(out=s_sb[0][:], in_=s_banks[0][:])
-        nc.scalar.copy(out=s_sb[1][:], in_=s_banks[1][:])
         val_sb = [keep.tile([P, S], F32, name="val%d" % t, align_bytes=64) for t in range(PACK)]
         nc.vector.tensor_copy(out=val_sb[0][:, first], in_=val_first[:, first])
         nc.vector.tensor_copy(out=val_sb[0][:, second], in_=val_banks[0][:, second])
-        w1s_late = keep.tile([P, P], U8, name="w1s_late", tag="w2_bf", align_bytes=64)
+        w1s_late = keep.tile([P, P], U8, name="w1s_late", tag="w2_bf1", align_bytes=64)
         deal_fours(nc, w1s_late, w1s_raw, slice(PACK - 1, PACK))
-        s_banks.append(project_s(PACK - 1, w1s_late[:]))
+        s_banks.append(project_s(PACK - 1, w1s_late[:], S_BANKS[PACK - 1]))
 
         def add_turned(acc, terms):
             for k in range(LISTS):
@@ -193,9 +202,10 @@ def tile_picked_aftlocal_none_po_kernel(
             for k in range(LISTS):
                 nc.scalar.activation(e[k][:], s_sb[t][:].indirect(lists[k][:]), ACT.Exp)
                 if k == 0 and t in (1, 2):
-                    nc.scalar.copy(out=s_sb[t + 1][:], in_=s_banks[t + 1][:])
+                    tokens = first if t == 1 else slice(0, S)
+                    nc.scalar.copy(out=s_sb[t + 1][:, tokens], in_=s_banks[t + 1][:, tokens])
                 if k == 1 and t == 1:
-                    nc.scalar.copy(out=val_sb[PACK - 1][:, : S // 4], in_=val_banks[PACK - 1][:, : S // 4])
+                    nc.scalar.copy(out=val_sb[PACK - 1][:, first], in_=val_banks[PACK - 1][:, first])
             val_t = val_sb[t]
             if last:
                 for h in range(HALVES):
@@ -204,7 +214,7 @@ def tile_picked_aftlocal_none_po_kernel(
                 for k in range(LISTS):
                     nc.vector.tensor_tensor(ev[k][:], val_t[:].indirect(lists[k][:]), e[k][:], MULT)
                     if k == 1:
-                        rest = slice(S // 4 if t + 1 == PACK - 1 else 0, S)
+                        rest = second if t + 1 == PACK - 1 else slice(0, S)
                         nc.vector.tensor_copy(out=val_sb[t + 1][:, rest], in_=val_banks[t + 1][:, rest])
                 for h in range(HALVES):
                     add_turned(den[h][:, tile_cols(t)], [e[k][:, tile_cols(h)] for k in range(LISTS)])

from contextlib import ExitStack

import concourse.mybir as mybir
from concourse.masks import make_identity

K, T, S, V, N, H = 512, 2048, 512, 256, 512, 512
FLOPS = 2 * K * H * S * 2 + 2 * H * N * V

F32 = mybir.dt.float32
BF16 = mybir.dt.bfloat16
I32 = mybir.dt.int32
U32 = mybir.dt.uint32
U16 = mybir.dt.uint16
U8 = mybir.dt.uint8
FP8X4 = mybir.dt.float8_e4m3fn_x4
FP4X4 = mybir.dt.float4_e2m1fn_x4
ACT = mybir.ActivationFunctionType
MULT = mybir.AluOpType.mult

P = 128
PACK = 4
LISTS = 3
QUADRANTS = 4
STRIPE = 16
HALVES = V // P
W2_PIECES = (slice(0, H // 2), slice(H // 2, 13 * H // 16), slice(13 * H // 16, H))
PAIRS = 2

S_BANKS = (0, 1, 2, 3)
VAL_BANKS = (4, 5, 6, 7)
DEN_BANKS = (4, 5)
NUM_BANKS = (0, 1)
TURN_BANKS = (2, 3)
Y_BANKS = ((6, 7), (4, 5))


def load_scale_rows(queues, plane, rows):
    for r in range(PACK):
        queues[r % len(queues)].dma_start(
            out=plane[r:P:32, :].bitcast(I32), in_=rows[r : QUADRANTS * PACK : PACK, :].bitcast(I32)
        )


def deal_words(nc, dealt, raw, tiles):
    nc.scalar.copy(
        out=dealt[:].bitcast(U16).rearrange("p (t a m) -> p a t m", t=tiles.stop - tiles.start, m=8),
        in_=raw[:].bitcast(U16).rearrange("p (a m t) -> p a t m", t=PACK, m=8)[:, :, tiles],
    )


def deal_scales(nc, dealt, raw):
    nc.vector.tensor_copy(
        out=dealt[:].rearrange("p (t a m) -> p a t m", t=PACK, m=16),
        in_=raw[:].rearrange("p (a m t) -> p a t m", t=PACK, m=16),
    )


def deal_fours(nc, dealt, raw, tiles=slice(0, PACK)):
    nc.vector.tensor_copy(
        out=dealt[:].bitcast(I32).rearrange("p (t a b w) -> p a t b w", t=tiles.stop - tiles.start, a=8, b=4),
        in_=raw[:].bitcast(I32).rearrange("p (a b t w) -> p a t b w", t=PACK, a=8, b=4)[:, :, tiles],
    )


def tile_picked_aftlocal_none_po_kernel(
    tc, x_words, x_scales, w1_words, w1_scales, w2, w3_words, w3_scales, offs, p1, p2, p3, out_0, out_1, out_2
):
    nc = tc.nc
    with ExitStack() as ctx:
        keep = ctx.enter_context(tc.tile_pool(name="keep", bufs=1))
        psum = ctx.enter_context(tc.psum_pool(name="psum", bufs=1))

        def in_bank(b, name):
            return psum.tile([P, S], F32, name=name, tag="bank%d" % b)

        def tile_cols(t, width=P):
            return slice(width * t, width * (t + 1))

        offs_t = keep.tile([P, S // STRIPE], U16, name="offs_t")
        lists = [keep.tile([P, V // STRIPE], U16, name="list%d" % k) for k in range(LISTS)]
        xw = keep.tile([P, T], U32, name="xw", align_bytes=64)
        xs = keep.tile([P, T], U8, name="xs", align_bytes=64)
        w1w_raw = keep.tile([P, 2 * H], U8, name="w1w_raw", align_bytes=64)
        w3w_raw = keep.tile([P, 2 * N], U8, name="w3w_raw", align_bytes=64)
        w1s_raw = keep.tile([P, H], U8, name="w1s_raw", align_bytes=64)
        w3s_raw = keep.tile([P, N], U8, name="w3s_raw", align_bytes=64)
        w2_raw = [
            keep.tile([P, PACK, piece.stop - piece.start], F32, name="w2_raw%d" % b, tag="w2_raw%d" % b, align_bytes=64)
            for b, piece in enumerate(W2_PIECES)
        ]
        ident = keep.tile([P, P], F32, name="ident", align_bytes=64)

        nc.vector.memset(xs[:].bitcast(I32), 0)
        nc.vector.memset(w1s_raw[:].bitcast(I32), 0)
        nc.vector.memset(w3s_raw[:].bitcast(I32), 0)

        nc.sync.dma_start(offs_t[:], offs)
        nc.sync.dma_start(out=w1w_raw[:].bitcast(I32), in_=w1_words[0].bitcast(I32))
        nc.sync.dma_start(lists[0][:], p1)
        x_rows = x_words[0].rearrange("p n t -> p (n t)").bitcast(I32)
        load_scale_rows((nc.scalar, nc.sync), xs, x_scales[0])
        nc.sync.dma_start(out=xw[:].bitcast(I32), in_=x_rows)
        load_scale_rows((nc.sync,), w1s_raw, w1_scales[0])
        w2_rows = w2.rearrange("(p j) c -> p j c", j=PACK)
        for raw, piece in zip(w2_raw, W2_PIECES):
            nc.sync.dma_start(out=raw[:], in_=w2_rows[:, :, piece])
        nc.sync.dma_start(lists[1][:], p2)
        nc.sync.dma_start(lists[2][:], p3)
        nc.sync.dma_start(out=w3w_raw[:].bitcast(I32), in_=w3_words[0].bitcast(I32))
        load_scale_rows((nc.sync,), w3s_raw, w3_scales[0])
        make_identity(nc, ident[:])

        xg_s = keep.tile([P, S], U8, name="xg_s", align_bytes=64)
        xg_w = keep.tile([P, S], U32, name="xg_w", align_bytes=64)
        w1w = keep.tile([P, 2 * H], U8, name="w1w", align_bytes=64)
        w2_bf = [
            keep.tile([P, PACK, P // 2, PACK], BF16, name="w2_bf%d" % g, tag="w2_bf%d" % g, align_bytes=64)
            for g in range(2)
        ]
        w1s_early = keep.tile([P, (PACK - 1) * P], U8, name="w1s_early", align_bytes=64)
        nc.vector.tensor_copy(xg_s[:], xs[:].indirect(offs_t[:]))
        deal_fours(nc, w1w, w1w_raw)
        nc.vector.tensor_copy(xg_w[:], xw[:].indirect(offs_t[:]))
        deal_fours(nc, w1s_early, w1s_raw, slice(0, PACK - 1))

        def project(bank, codes, scales, tokens=slice(0, S)):
            nc.tensor.matmul_mx(
                out=bank[:, tokens],
                lhsT=codes,
                lhsT_scale=scales,
                rhs=xg_w[:, tokens].bitcast(FP8X4),
                rhs_scale=xg_s[:, tokens],
                start=True,
                stop=True,
            )
            return bank

        s_sb = [keep.tile([P, S], F32, name="s%d" % t, align_bytes=64) for t in range(PACK)]

        w2q = keep.tile([P, H], U32, name="w2q", align_bytes=64)
        w2s = keep.tile([P, H], U8, name="w2s", align_bytes=64)

        def round_w2(b, tiles):
            g, start = divmod(W2_PIECES[b].start, H // 2)
            columns = slice(start // PACK, (W2_PIECES[b].stop - g * H // 2) // PACK)
            nc.vector.tensor_copy(
                out=w2_bf[g][:, tiles, columns, :].rearrange("p t (q c) j -> p t q j c", c=PACK),
                in_=w2_raw[b][:].rearrange("p j (q t c) -> p t q j c", t=PACK, c=PACK)[:, tiles],
            )

        def quantize_w2(g, t):
            columns = slice(P * t + P // 2 * g, P * t + P // 2 * (g + 1))
            nc.vector.quantize_mx(
                out=w2q[:, columns].bitcast(FP8X4),
                scales=w2s[:, columns],
                in_=w2_bf[g][:, t].rearrange("p m j -> p (m j)"),
            )

        round_w2(0, slice(0, PACK))
        round_w2(1, slice(0, PACK))
        for t in range(PACK):
            quantize_w2(0, t)
        round_w2(2, slice(0, 1))
        round_w2(2, slice(1, PACK))
        for t in range(PACK):
            quantize_w2(1, t)

        def project_s(t, scales, bank, tokens=slice(0, S)):
            w1_codes = w1w[:, tile_cols(t, 2 * P)].bitcast(FP4X4)
            return project(in_bank(bank, "s_acc"), w1_codes, scales, tokens)

        first, second = slice(0, S // 2), slice(S // 2, S)
        s_banks = [project_s(t, w1s_early[:, tile_cols(t)], S_BANKS[t]) for t in range(2)]
        s_banks.append(project_s(2, w1s_early[:, tile_cols(2)], S_BANKS[2], first))
        nc.scalar.copy(out=s_sb[0][:], in_=s_banks[0][:])
        nc.scalar.copy(out=s_sb[1][:], in_=s_banks[1][:])
        s2_second = project_s(2, w1s_early[:, tile_cols(2)], S_BANKS[0], second)
        nc.vector.tensor_copy(out=s_sb[2][:, second], in_=s2_second[:, second])

        def project_val(t, bank, tokens):
            return project(in_bank(bank, "val_acc"), w2q[:, tile_cols(t)].bitcast(FP8X4), w2s[:, tile_cols(t)], tokens)

        val_first = project_val(0, S_BANKS[PACK - 1], first)
        val_banks = [project_val(t, VAL_BANKS[t], second if t == 0 else slice(0, S)) for t in range(PACK)]
        val_sb = [keep.tile([P, S], F32, name="val%d" % t, align_bytes=64) for t in range(PACK)]
        nc.vector.tensor_copy(out=val_sb[0][:, first], in_=val_first[:, first])
        nc.vector.tensor_copy(out=val_sb[0][:, second], in_=val_banks[0][:, second])
        w1s_late = keep.tile([P, P], U8, name="w1s_late", tag="w2_bf1", align_bytes=64)
        deal_fours(nc, w1s_late, w1s_raw, slice(PACK - 1, PACK))
        s_banks.append(project_s(PACK - 1, w1s_late[:], S_BANKS[PACK - 1]))

        def add_turned(acc, terms):
            for k in range(LISTS):
                nc.tensor.matmul(acc, terms[k], ident[:], start=(k == 0), stop=(k == LISTS - 1), is_transpose=True)

        den = [in_bank(DEN_BANKS[h], "den") for h in range(HALVES)]
        num = [in_bank(NUM_BANKS[h], "num") for h in range(HALVES)]
        for t in range(PACK):
            last = t == PACK - 1
            e = [keep.tile([P, V], F32, name="e%d_%d" % (t, k), align_bytes=64) for k in range(LISTS)]
            ev = [keep.tile([P, V], F32, name="ev%d_%d" % (t, k), align_bytes=64) for k in range(LISTS)]
            for k in range(LISTS):
                nc.scalar.activation(e[k][:], s_sb[t][:].indirect(lists[k][:]), ACT.Exp)
                if k == 0 and t in (1, 2):
                    tokens = first if t == 1 else slice(0, S)
                    nc.scalar.copy(out=s_sb[t + 1][:, tokens], in_=s_banks[t + 1][:, tokens])
                if k == 1 and t == 1:
                    nc.scalar.copy(out=val_sb[PACK - 1][:, first], in_=val_banks[PACK - 1][:, first])
            val_t = val_sb[t]
            if last:
                for h in range(HALVES):
                    add_turned(den[h][:, tile_cols(t)], [e[k][:, tile_cols(h)] for k in range(LISTS)])
            if not last:
                for k in range(LISTS):
                    nc.vector.tensor_tensor(ev[k][:], val_t[:].indirect(lists[k][:]), e[k][:], MULT)
                    if k == 1:
                        rest = second if t + 1 == PACK - 1 else slice(0, S)
                        nc.vector.tensor_copy(out=val_sb[t + 1][:, rest], in_=val_banks[t + 1][:, rest])
                for h in range(HALVES):
                    add_turned(den[h][:, tile_cols(t)], [e[k][:, tile_cols(h)] for k in range(LISTS)])
                for h in range(HALVES):
                    add_turned(num[h][:, tile_cols(t)], [ev[k][:, tile_cols(h)] for k in range(LISTS)])
            else:
                for h in range(HALVES):
                    places = tile_cols(h)
                    for k in range(LISTS):
                        offsets = lists[k][:, tile_cols(h, P // STRIPE)]
                        nc.vector.tensor_tensor(ev[k][:, places], val_t[:].indirect(offsets), e[k][:, places], MULT)
                    add_turned(num[h][:, tile_cols(t)], [ev[k][:, places] for k in range(LISTS)])


        y = [keep.tile([P, PACK, P], F32, name="y%d" % h, align_bytes=64) for h in range(HALVES)]
        y_words = keep.tile([P, V], U32, name="y_words", align_bytes=64)
        y_scales = keep.tile([P, V], U8, name="y_scales", align_bytes=64)
        out_rows = out_0.rearrange("(p t) v -> p t v", t=PACK)
        out_words = out_1[0].rearrange("p v r -> p (v r)").bitcast(I32)

        def pair_of_sums(acc, u):
            return acc[:].rearrange("v (t q u d) -> v u q t d", t=PACK, u=PAIRS, d=2)[:, u]

        def like_sums(row):
            return row.rearrange("v (q t d) -> v q t d", t=PACK, d=2)

        roots, step = [], []
        for h in range(HALVES):
            roots.append(keep.tile([P, H], F32, name="root%d" % h, align_bytes=64))
            step.append([keep.tile([P, 2 * P], F32, name="other%d_%d" % (h, u), align_bytes=64) for u in range(PAIRS)])
            for u in range(PAIRS):
                pair = tile_cols(u, 2 * P)
                nc.scalar.activation(like_sums(roots[h][:, pair]), pair_of_sums(den[h], u), ACT.Abs_reciprocal_sqrt)
                if h == 0:
                    nc.vector.tensor_tensor(
                        like_sums(step[h][u][:]), pair_of_sums(num[h], u), like_sums(roots[h][:, pair]), MULT
                    )
                else:
                    nc.scalar.activation(step[h][u][:], roots[h][:, pair], ACT.Square)

        turned = []
        for h in range(HALVES):
            z_turned = keep.tile([P, H], BF16, name="z_turned%d" % h, tag="z_turned%d" % h, align_bytes=64)
            z_pairs = in_bank(TURN_BANKS[h], "z_pairs")
            turned.append(z_pairs)
            for u in range(PAIRS):
                pair = tile_cols(u, 2 * P)
                if h == 0:
                    nc.vector.tensor_tensor(z_turned[:, pair], step[h][u][:], roots[h][:, pair], MULT)
                else:
                    nc.vector.tensor_tensor(
                        like_sums(z_turned[:, pair]), pair_of_sums(num[h], u), like_sums(step[h][u][:]), MULT
                    )
                nc.tensor.transpose(z_pairs[:, tile_cols(u)], z_turned[:, pair].bitcast(F32), ident[:])

        w3w = [keep.tile([P, N], U8, name="w3w0", tag="root0", align_bytes=64)]
        deal_words(nc, w3w[0], w3w_raw, slice(0, 2))
        w3s = keep.tile([P, N], U8, name="w3s", tag="other1_0", align_bytes=64)
        deal_scales(nc, w3s, w3s_raw)

        y_bf = [keep.tile([P, P, PACK], BF16, name="y_bf%d" % h, align_bytes=64) for h in range(HALVES)]
        for h in range(HALVES):
            places = tile_cols(h)
            z_pairs = turned[h]
            z_bf = keep.tile([P, P * PACK], BF16, name="z_bf%d" % h, align_bytes=64)
            nc.scalar.copy(
                out=z_bf[:].bitcast(F32).rearrange("p (v u) -> p v u", u=PAIRS),
                in_=z_pairs[:, 0 : 2 * P].rearrange("p (u v) -> p v u", u=PAIRS),
            )
            if h == 0:
                w3w.append(keep.tile([P, N], U8, name="w3w1", tag="z_turned0", align_bytes=64))
                deal_words(nc, w3w[1], w3w_raw, slice(2, PACK))
            zq = keep.tile([P, P], U32, name="zq%d" % h, align_bytes=64)
            zs = keep.tile([P, P], U8, name="zs%d" % h, align_bytes=64)
            nc.vector.quantize_mx(out=zq[:].bitcast(FP8X4), scales=zs[:], in_=z_bf[:])

            for b, bank in enumerate(Y_BANKS[h]):
                y_acc = in_bank(bank, "y_acc")
                for i in range(2):
                    t = 2 * b + i
                    nc.tensor.matmul_mx(
                        out=y_acc[:, tile_cols(i)],
                        lhsT=w3w[b][:, tile_cols(i, 2 * P)].bitcast(FP4X4),
                        lhsT_scale=w3s[:, tile_cols(t)],
                        rhs=zq[:].bitcast(FP8X4),
                        rhs_scale=zs[:],
                        start=True,
                        stop=True,
                    )
                if (h, b) == (1, 1):
                    nc.scalar.copy(
                        out=y_bf[h][:, :, 2 * b : 2 * b + 2], in_=y_acc[:, 0 : 2 * P].rearrange("p (t v) -> p v t", t=2)
                    )
                copy = nc.vector.tensor_copy if (h, b) == (0, 0) else nc.scalar.copy
                copy(out=y[h][:, 2 * b : 2 * b + 2, :], in_=y_acc[:, 0 : 2 * P].rearrange("p (t v) -> p t v", t=2))
        nc.sync.dma_start(out=out_rows[:, :, 0:P], in_=y[0][:])
        for b in range(2):
            nc.sync.dma_start(out=out_rows[:, 2 * b : 2 * b + 2, P:V], in_=y[1][:, 2 * b : 2 * b + 2, :])

        nc.vector.tensor_copy(
            out=y_bf[0][:].rearrange("p (c i) t -> p c t i", i=4), in_=y[0][:].rearrange("p t (c i) -> p c t i", i=4)
        )
        nc.vector.tensor_copy(out=y_bf[1][:, :, 0:2], in_=y[1][:, 0:2, :].rearrange("p t v -> p v t"))
        for h in range(HALVES):
            places = tile_cols(h)
            nc.vector.quantize_mx(
                out=y_words[:, places].bitcast(FP8X4),
                scales=y_scales[:, places],
                in_=y_bf[h][:].rearrange("p v t -> p (v t)"),
            )
        nc.sync.dma_start(out=out_words, in_=y_words[:].bitcast(I32))

        for q in range(QUADRANTS):
            queue = (nc.sync, nc.scalar)[q % 2]
            queue.dma_start(
                out=out_2[0][4 * q : 4 * q + 4, :].bitcast(I32), in_=y_scales[32 * q : 32 * q + 4, :].bitcast(I32)
            )
